import numpy as np
import ml_dtypes


def mxq(x, axis, fmt="e4m3"):
    dtype, down = {"e4m3": (ml_dtypes.float8_e4m3fn, 7), "e5m2": (ml_dtypes.float8_e5m2, 14)}[fmt]
    v = np.moveaxis(np.asarray(x, np.float32).astype(ml_dtypes.bfloat16).astype(np.float64), axis, -1)
    blocks = v.reshape(v.shape[:-1] + (-1, 32))
    amax = np.abs(blocks).max(-1, keepdims=True)
    byte = np.maximum(np.where(amax > 0, np.frexp(amax)[1] - 1 + 127, 0) - down, 1)
    scale = np.exp2(byte - 127.0)
    codes = (blocks / scale).astype(np.float32).astype(dtype).astype(np.float64)
    return np.moveaxis((codes * scale).reshape(v.shape), -1, axis)


WIDE = False


def mx_kscale(k):
    if not WIDE:
        return np.ones(k)
    levels = np.array([10, -10, 5, -5, 0])
    if k % 512:
        return np.exp2(np.random.permutation(np.resize(levels, k // 32))).repeat(32)
    a = np.empty((k // 512, 16))
    for p in range(k // 512):
        a[p, :8] = np.random.permutation(np.resize(levels, 8))
        for g in range(8):
            far = levels[np.abs(levels - a[p, g]) >= 10]
            a[p, g + 8] = far[np.random.randint(len(far))]
    return np.exp2(a.ravel()).repeat(32)


def f64(x):
    return np.asarray(x).astype(np.float64)


def striped8(idx):
    return np.concatenate([v.reshape(-1, 16).T for v in idx]).astype(np.uint16)


def unstriped8(offs):
    return np.stack([offs[16 * g:16 * g + 16].T.reshape(-1) for g in range(8)]).astype(np.int64)


E2M1 = np.array([0.0, 0.5, 1.0, 1.5, 2.0, 3.0, 4.0, 6.0, -0.0, -0.5, -1.0, -1.5, -2.0, -3.0, -4.0, -6.0])


def pack_weight(w, fmt):
    k, n = w.shape
    w = f64(np.asarray(w, np.float32).astype(ml_dtypes.bfloat16)).reshape(k // 32, 32, n)
    amax = np.abs(w).max(1)
    if fmt == "e4m3":
        byte = np.frexp(amax)[1] - 1 + 127 - 7
    else:
        mant, ex = np.frexp(amax / 6.0)
        byte = np.where(mant > 0.5, ex, ex - 1) + 127
    byte = np.clip(np.where(amax > 0, byte, 1), 1, 254)
    scaled = (w * np.exp2(127.0 - byte)[:, None, :]).reshape(k, n).astype(np.float32)
    by_word = np.ascontiguousarray(scaled.reshape(k // 512, 128, 4, n).transpose(0, 1, 3, 2))
    if fmt == "e4m3":
        words = by_word.astype(ml_dtypes.float8_e4m3fn).view(np.uint8)
    else:
        c = by_word.astype(ml_dtypes.float4_e2m1fn).view(np.uint8) & 0xF
        words = (c[..., 0::2] | (c[..., 1::2] << 4)).reshape(k // 512, 128, 2 * n)
    return np.ascontiguousarray(words), np.ascontiguousarray(byte.astype(np.uint8).reshape(k // 512, 16, n))


def unpack_weight(words, scales, fmt):
    g, _, n = scales.shape
    words = np.ascontiguousarray(words).reshape(g, 128, n, -1)
    if fmt == "e4m3":
        vals = words.view(ml_dtypes.float8_e4m3fn).astype(np.float64)
    else:
        nib = np.empty((g, 128, n, 4), np.uint8)
        nib[..., 0::2] = words & 0xF
        nib[..., 1::2] = words >> 4
        vals = E2M1[nib]
    vals = vals * np.repeat(np.exp2(scales.astype(np.float64) - 127.0), 8, axis=1)[..., None]
    return vals.transpose(0, 1, 3, 2).reshape(g * 512, n)


def silu(v):
    return v / (1.0 + np.exp(-np.maximum(v, -700.0)))


K, M, T, S = 512, 512, 1024, 512


def setup_inputs():
    n = np.random.standard_normal
    s = mx_kscale(K)[:, None]
    s2 = mx_kscale(512)[:, None]
    p_w4 = pack_weight(n((K, M)) / np.sqrt(K) / s, "e2m1")
    return {
        "xT": (n((K, T)) * s).astype(np.float32),
        "w4_words": p_w4[0],
        "w4_scales": p_w4[1],
        "c": (n((512, S)) * s2).astype(np.float32),
        "u": (n((512, M)) / np.sqrt(512) / s2).astype(np.float32),
        "wgt": np.repeat(np.random.uniform(0.5, 2.0, (8, S)), 16, axis=0).astype(np.float32),
        "b": (0.3 * n(512)).astype(np.float32),
        "wgo": np.repeat(np.random.uniform(0.5, 2.0, (8, S)), 16, axis=0).astype(np.float32),
        "offs": striped8(np.stack([np.random.permutation(T)[:S] for _ in range(8)])),
        "offs2": striped8(np.stack([np.random.permutation(T)[:S] for _ in range(8)])),
    }


def reference(xT, w4_words, w4_scales, c, u, wgt, b, wgo, offs, offs2):
    idx = unstriped8(offs)
    group = np.arange(K) % 512 // 64
    xg = f64(wgt)[np.arange(K) // 4 % 128] * f64(xT)[np.arange(K)[:, None], idx[group]]
    xT_ = mxq(xg, 0, "e4m3")
    w4_ = unpack_weight(w4_words, w4_scales, "e2m1")
    c_ = mxq(f64(c), 0, "e4m3")
    u_ = mxq(f64(u), 0, "e4m3")
    y = w4_.T @ xT_ + u_.T @ c_
    place = unstriped8(offs2)[np.arange(M) % 128 // 16]
    out = np.zeros((M, T))
    out[np.arange(M)[:, None], place] = f64(wgo)[np.arange(M) % 128] * (silu(y + f64(b)[:, None]))
    return out

@@ -1,0 +1,165 @@
+from contextlib import ExitStack
+
+import concourse.mybir as mybir
+
+K, M, T, S = 512, 512, 1024, 512
+FLOPS = 2 * 2 * K * M * S
+
+F32 = mybir.dt.float32
+BF16 = mybir.dt.bfloat16
+I32 = mybir.dt.int32
+U32 = mybir.dt.uint32
+U16 = mybir.dt.uint16
+U8 = mybir.dt.uint8
+FP8X4 = mybir.dt.float8_e4m3fn_x4
+FP4X4 = mybir.dt.float4_e2m1fn_x4
+MULT = mybir.AluOpType.mult
+SILU = mybir.ActivationFunctionType.Silu
+
+P = 128
+PACK = 4
+HALF = S // 2
+N_PASS = 128
+LIST_COLS = HALF // 16
+
+
+def tile_list_hboth_d_silu_kernel(tc, xT, w4_words, w4_scales, c, u, wgt, b, wgo, offs, offs2, out):
+    nc = tc.nc
+    with ExitStack() as ctx:
+        sb = ctx.enter_context(tc.tile_pool(name="sb", bufs=1))
+        psum = ctx.enter_context(tc.psum_pool(name="psum", bufs=1))
+
+        gather_list = sb.tile([P, S // 16], U16, name="gather_list")
+        scatter_list = sb.tile([P, S // 16], U16, name="scatter_list")
+        wgt_sb = sb.tile([P, S], F32, name="wgt_sb")
+        wgo_sb = sb.tile([P, S], F32, name="wgo_sb")
+        planes = [sb.tile([P, T], F32, name=f"plane{i}") for i in range(PACK)]
+        windows = [sb.tile([P, T], F32, name=f"window{t}") for t in range(M // P)]
+        w4_sb = sb.tile([P, 2 * M], U8, name="w4_sb", align_bytes=64)
+        w4_scale = sb.tile([P, M], U8, name="w4_scale", align_bytes=64)
+        bias = sb.tile([P, M // P], F32, name="bias")
+        warm = sb.tile([P, 8], F32, name="warm")
+        warm_out = sb.tile([P, 8], F32, name="warm_out")
+
+        def operand(name, width):
+            return {
+                "raw": sb.tile([P, PACK, width], F32, name=name + "_raw"),
+                "bf": sb.tile([P, width, PACK], BF16, name=name + "_bf", align_bytes=64),
+                "codes": sb.tile([P, width], U32, name=name + "_codes", align_bytes=64),
+                "scale": sb.tile([P, width], U8, name=name + "_scale", align_bytes=64),
+            }
+
+        xg = [operand(f"xg{h}", HALF) for h in range(2)]
+        cq = [operand(f"c{h}", HALF) for h in range(2)]
+        u0 = operand("u0", P)
+        u1 = operand("u1", P)
+        u23 = operand("u23", 2 * P)
+        u_of = [(u0, 0), (u1, 0), (u23, 0), (u23, P)]
+
+        x_rows = xT.rearrange("(p i) t -> p i t", i=PACK)
+        c_rows = c.rearrange("(p i) j -> p i j", i=PACK)
+        u_rows = u.rearrange("(p i) n -> p i n", i=PACK)
+
+        def half(h):
+            return slice(h * HALF, (h + 1) * HALF)
+
+        def list_half(h):
+            return slice(h * LIST_COLS, (h + 1) * LIST_COLS)
+
+        nc.gpsimd.memset(warm[:], 0.0)
+        nc.scalar.activation(warm_out[:], warm[:], SILU)
+        nc.gpsimd.memset(w4_scale[:].bitcast(I32), 0)
+        for q in range(4):
+            nc.gpsimd.dma_start(w4_scale[32 * q : 32 * q + 4, :].bitcast(I32), w4_scales[0, 4 * q : 4 * q + 4, :].bitcast(I32))
+        with nc.allow_non_contiguous_dma(reason="one bias value for each partition and row tile"):
+            nc.gpsimd.dma_start(bias[:], b.rearrange("(t p) -> p t", p=P))
+
+        nc.sync.dma_start(gather_list[:], offs)
+        nc.sync.dma_start(wgt_sb[:], wgt)
+        for i in range(PACK):
+            nc.sync.dma_start(planes[i][:], x_rows[:, i, :])
+        nc.sync.dma_start(cq[0]["raw"][:], c_rows[:, :, half(0)])
+        nc.sync.dma_start(u0["raw"][:], u_rows[:, :, 0:P])
+        nc.sync.dma_start(w4_sb[:].bitcast(I32), w4_words[0].bitcast(I32))
+        nc.sync.dma_start(u1["raw"][:], u_rows[:, :, P : 2 * P])
+        nc.sync.dma_start(scatter_list[:], offs2)
+        nc.sync.dma_start(wgo_sb[:], wgo)
+        nc.sync.dma_start(u23["raw"][:], u_rows[:, :, 2 * P : 4 * P])
+        nc.sync.dma_start(cq[1]["raw"][:], c_rows[:, :, half(1)])
+
+        for window in windows:
+            nc.vector.memset(window[:], 0.0)
+
+        def gather(i, h):
+            nc.vector.tensor_tensor(xg[h]["raw"][:, i, :], planes[i][:].indirect(gather_list[:, list_half(h)]), wgt_sb[:, half(h)], MULT)
+
+        def interleave(copy, op):
+            copy(op["bf"][:].rearrange("p (c r) i -> p c i r", r=4), op["raw"][:].rearrange("p i (c r) -> p c i r", r=4))
+
+        def quantize(op):
+            nc.vector.quantize_mx(out=op["codes"][:].bitcast(FP8X4), scales=op["scale"][:], in_=op["bf"][:].rearrange("p w i -> p (w i)"))
+
+        acts = {}
+
+        def project(t, h):
+            acc = psum.tile([P, HALF], F32, name=f"acc{t}_{h}")
+            u_op, u_at = u_of[t]
+            for j0 in range(0, HALF, N_PASS):
+                cols = slice(j0, j0 + N_PASS)
+                nc.tensor.matmul_mx(
+                    out=acc[:, cols],
+                    lhsT=w4_sb[:, 2 * P * t : 2 * P * (t + 1)].bitcast(FP4X4),
+                    lhsT_scale=w4_scale[:, P * t : P * (t + 1)],
+                    rhs=xg[h]["codes"][:, cols].bitcast(FP8X4),
+                    rhs_scale=xg[h]["scale"][:, cols],
+                    start=True,
+                    stop=False,
+                )
+                nc.tensor.matmul_mx(
+                    out=acc[:, cols],
+                    lhsT=u_op["codes"][:, u_at : u_at + P].bitcast(FP8X4),
+                    lhsT_scale=u_op["scale"][:, u_at : u_at + P],
+                    rhs=cq[h]["codes"][:, cols].bitcast(FP8X4),
+                    rhs_scale=cq[h]["scale"][:, cols],
+                    start=False,
+                    stop=True,
+                )
+            act = sb.tile([P, HALF], F32, name=f"act{t}_{h}")
+            nc.scalar.activation(act[:], acc[:], SILU, bias=bias[:, t : t + 1])
+            acts.setdefault((t, h), act)
+
+        def scatter(t, h):
+            nc.vector.tensor_tensor(windows[t][:].indirect(scatter_list[:, list_half(h)]), acts[(t, h)][:], wgo_sb[:, half(h)], MULT)
+
+        for i in range(PACK - 1):
+            gather(i, 0)
+            gather(i, 1)
+        gather(3, 0)
+        interleave(nc.scalar.copy, xg[0])
+        gather(3, 1)
+        interleave(nc.scalar.copy, xg[1])
+        interleave(nc.vector.tensor_copy, cq[0])
+        quantize(xg[0])
+        quantize(cq[0])
+        interleave(nc.vector.tensor_copy, u0)
+        quantize(u0)
+        project(0, 0)
+        interleave(nc.vector.tensor_copy, u1)
+        quantize(xg[1])
+        quantize(u1)
+        project(1, 0)
+        interleave(nc.scalar.copy, u23)
+        scatter(0, 0)
+        quantize(u23)
+        project(2, 0)
+        project(3, 0)
+        interleave(nc.scalar.copy, cq[1])
+        scatter(1, 0)
+        quantize(cq[1])
+        for t in range(M // P):
+            project(t, 1)
+        scatter(2, 0)
+        scatter(3, 0)
+        for t in range(M // P):
+            scatter(t, 1)
+            nc.sync.dma_start(out[P * t : P * (t + 1), :], windows[t][:])

@@ -1,6 +1,7 @@
 from contextlib import ExitStack
 
 import concourse.mybir as mybir
+from concourse.masks import make_identity
 
 K, M, T, S = 512, 512, 1024, 512
 FLOPS = 2 * 2 * K * M * S
@@ -38,23 +39,29 @@ def tile_list_hboth_d_silu_kernel(tc, xT, w4_words, w4_scales, c, u, wgt, b, wgo
         w4_sb = sb.tile([P, 2 * M], U8, name="w4_sb", align_bytes=64)
         w4_scale = sb.tile([P, M], U8, name="w4_scale", align_bytes=64)
         bias = sb.tile([P, M // P], F32, name="bias")
+        bias_rows = sb.tile([P, P], F32, name="bias_rows")
+        identity = sb.tile([P, P], F32, name="identity")
         warm = sb.tile([P, 8], F32, name="warm")
         warm_out = sb.tile([P, 8], F32, name="warm_out")
 
+        def raw_tile(name, width):
+            return sb.tile([P, PACK, width], F32, name=name + "_raw")
+
         def operand(name, width):
             return {
-                "raw": sb.tile([P, PACK, width], F32, name=name + "_raw"),
-                "bf": sb.tile([P, width, PACK], BF16, name=name + "_bf", align_bytes=64),
                 "codes": sb.tile([P, width], U32, name=name + "_codes", align_bytes=64),
                 "scale": sb.tile([P, width], U8, name=name + "_scale", align_bytes=64),
             }
 
+        xg_raw = [raw_tile(f"xg{h}", HALF) for h in range(2)]
+        c_raw = [raw_tile(f"c{h}", HALF) for h in range(2)]
+        u0_raw = sb.tile([P, PACK, P], F32, name="u0_raw", tag="after_u0", align_bytes=64)
+        u1_raw = raw_tile("u1", P)
+        u23_raw = raw_tile("u23", 2 * P)
         xg = [operand(f"xg{h}", HALF) for h in range(2)]
         cq = [operand(f"c{h}", HALF) for h in range(2)]
-        u0 = operand("u0", P)
-        u1 = operand("u1", P)
-        u23 = operand("u23", 2 * P)
-        u_of = [(u0, 0), (u1, 0), (u23, 0), (u23, P)]
+        uq = [operand(f"u{t}", P) for t in range(M // P)]
+        first_bias = sb.tile([P, 1], F32, name="first_bias", tag="after_first_silu", align_bytes=64)
 
         x_rows = xT.rearrange("(p i) t -> p i t", i=PACK)
         c_rows = c.rearrange("(p i) j -> p i j", i=PACK)
@@ -66,44 +73,55 @@ def tile_list_hboth_d_silu_kernel(tc, xT, w4_words, w4_scales, c, u, wgt, b, wgo
         def list_half(h):
             return slice(h * LIST_COLS, (h + 1) * LIST_COLS)
 
-        nc.gpsimd.memset(warm[:], 0.0)
-        nc.scalar.activation(warm_out[:], warm[:], SILU)
         nc.gpsimd.memset(w4_scale[:].bitcast(I32), 0)
+        nc.gpsimd.memset(bias_rows[:], 0.0)
+        nc.gpsimd.memset(warm[:], 0.0)
         for q in range(4):
-            nc.gpsimd.dma_start(w4_scale[32 * q : 32 * q + 4, :].bitcast(I32), w4_scales[0, 4 * q : 4 * q + 4, :].bitcast(I32))
-        with nc.allow_non_contiguous_dma(reason="one bias value for each partition and row tile"):
-            nc.gpsimd.dma_start(bias[:], b.rearrange("(t p) -> p t", p=P))
+            nc.scalar.dma_start(w4_scale[32 * q : 32 * q + 4, :].bitcast(I32), w4_scales[0, 4 * q : 4 * q + 4, :].bitcast(I32))
+        nc.scalar.dma_start(bias_rows[0 : M // P, :], b.rearrange("(t p) -> t p", p=P))
+        nc.scalar.activation(warm_out[:], warm[:], SILU)
+        make_identity(nc, identity[:])
+        bias_ps = psum.tile([P, P], F32, name="acc3_1")
+        nc.tensor.transpose(bias_ps[:], bias_rows[:], identity[:])
+        nc.scalar.copy(bias[:], bias_ps[:, 0 : M // P])
+        nc.scalar.copy(first_bias[:], bias_ps[:, 0:1])
 
         nc.sync.dma_start(gather_list[:], offs)
         nc.sync.dma_start(wgt_sb[:], wgt)
         for i in range(PACK):
             nc.sync.dma_start(planes[i][:], x_rows[:, i, :])
-        nc.sync.dma_start(cq[0]["raw"][:], c_rows[:, :, half(0)])
-        nc.sync.dma_start(u0["raw"][:], u_rows[:, :, 0:P])
+        nc.sync.dma_start(c_raw[0][:], c_rows[:, :, half(0)])
+        nc.sync.dma_start(u0_raw[:], u_rows[:, :, 0:P])
         nc.sync.dma_start(w4_sb[:].bitcast(I32), w4_words[0].bitcast(I32))
-        nc.sync.dma_start(u1["raw"][:], u_rows[:, :, P : 2 * P])
+        nc.sync.dma_start(u1_raw[:], u_rows[:, :, P : 2 * P])
         nc.sync.dma_start(scatter_list[:], offs2)
-        nc.sync.dma_start(wgo_sb[:], wgo)
-        nc.sync.dma_start(u23["raw"][:], u_rows[:, :, 2 * P : 4 * P])
-        nc.sync.dma_start(cq[1]["raw"][:], c_rows[:, :, half(1)])
+        nc.sync.dma_start(wgo_sb[:, half(0)], wgo[:, half(0)])
+        nc.sync.dma_start(u23_raw[:], u_rows[:, :, 2 * P : 4 * P])
+        nc.sync.dma_start(c_raw[1][:], c_rows[:, :, half(1)])
+        nc.sync.dma_start(wgo_sb[:, half(1)], wgo[:, half(1)])
 
-        for window in windows:
+        for window in windows[:2]:
             nc.vector.memset(window[:], 0.0)
+        for window in windows[2:]:
+            nc.gpsimd.memset(window[:], 0.0)
 
         def gather(i, h):
-            nc.vector.tensor_tensor(xg[h]["raw"][:, i, :], planes[i][:].indirect(gather_list[:, list_half(h)]), wgt_sb[:, half(h)], MULT)
+            nc.vector.tensor_tensor(xg_raw[h][:, i, :], planes[i][:].indirect(gather_list[:, list_half(h)]), wgt_sb[:, half(h)], MULT)
 
-        def interleave(copy, op):
-            copy(op["bf"][:].rearrange("p (c r) i -> p c i r", r=4), op["raw"][:].rearrange("p i (c r) -> p c i r", r=4))
+        def interleave(copy, name, raw, tag=None):
+            width = raw.shape[2]
+            grouped = sb.tile([P, width, PACK], BF16, name=name, tag=tag or name, align_bytes=64)
+            copy(grouped[:].rearrange("p (c r) i -> p c i r", r=4), raw.rearrange("p i (c r) -> p c i r", r=4))
+            return grouped
 
-        def quantize(op):
-            nc.vector.quantize_mx(out=op["codes"][:].bitcast(FP8X4), scales=op["scale"][:], in_=op["bf"][:].rearrange("p w i -> p (w i)"))
+        def quantize(op, grouped, at=0):
+            cols = slice(at, at + grouped.shape[1])
+            nc.vector.quantize_mx(out=op["codes"][:, cols].bitcast(FP8X4), scales=op["scale"][:, cols], in_=grouped[:].rearrange("p w i -> p (w i)"))
 
         acts = {}
 
         def project(t, h):
             acc = psum.tile([P, HALF], F32, name=f"acc{t}_{h}")
-            u_op, u_at = u_of[t]
             for j0 in range(0, HALF, N_PASS):
                 cols = slice(j0, j0 + N_PASS)
                 nc.tensor.matmul_mx(
@@ -117,48 +135,55 @@ def tile_list_hboth_d_silu_kernel(tc, xT, w4_words, w4_scales, c, u, wgt, b, wgo
                 )
                 nc.tensor.matmul_mx(
                     out=acc[:, cols],
-                    lhsT=u_op["codes"][:, u_at : u_at + P].bitcast(FP8X4),
-                    lhsT_scale=u_op["scale"][:, u_at : u_at + P],
+                    lhsT=uq[t]["codes"][:].bitcast(FP8X4),
+                    lhsT_scale=uq[t]["scale"][:],
                     rhs=cq[h]["codes"][:, cols].bitcast(FP8X4),
                     rhs_scale=cq[h]["scale"][:, cols],
                     start=False,
                     stop=True,
                 )
             act = sb.tile([P, HALF], F32, name=f"act{t}_{h}")
-            nc.scalar.activation(act[:], acc[:], SILU, bias=bias[:, t : t + 1])
+            nc.scalar.activation(act[:], acc[:], SILU, bias=first_bias[:] if (t, h) == (0, 0) else bias[:, t : t + 1])
             acts.setdefault((t, h), act)
 
         def scatter(t, h):
             nc.vector.tensor_tensor(windows[t][:].indirect(scatter_list[:, list_half(h)]), acts[(t, h)][:], wgo_sb[:, half(h)], MULT)
 
+        on_scalar, on_vector = nc.scalar.copy, nc.vector.tensor_copy
         for i in range(PACK - 1):
             gather(i, 0)
             gather(i, 1)
         gather(3, 0)
-        interleave(nc.scalar.copy, xg[0])
+        xg0_bf = interleave(on_scalar, "xg0_bf", xg_raw[0][:])
         gather(3, 1)
-        interleave(nc.scalar.copy, xg[1])
-        interleave(nc.vector.tensor_copy, cq[0])
-        quantize(xg[0])
-        quantize(cq[0])
-        interleave(nc.vector.tensor_copy, u0)
-        quantize(u0)
+        c0_bf = interleave(on_vector, "c0_bf", c_raw[0][:])
+        u0_bf = interleave(on_scalar, "u0_bf", u0_raw[:])
+        quantize(xg[0], xg0_bf)
+        quantize(cq[0], c0_bf)
+        quantize(uq[0], u0_bf)
         project(0, 0)
-        interleave(nc.vector.tensor_copy, u1)
-        quantize(xg[1])
-        quantize(u1)
+        u1_bf = interleave(on_vector, "u1_bf", u1_raw[:])
+        quantize(uq[1], u1_bf)
         project(1, 0)
-        interleave(nc.scalar.copy, u23)
         scatter(0, 0)
-        quantize(u23)
+        u2_bf = interleave(on_scalar, "u2_bf", u23_raw[:, :, 0:P])
+        u3_bf = interleave(on_scalar, "u3_bf", u23_raw[:, :, P : 2 * P])
+        xg1a_bf = interleave(on_scalar, "xg1a_bf", xg_raw[1][:, :, 0:P], tag="after_u0")
+        xg1b_bf = interleave(on_scalar, "xg1b_bf", xg_raw[1][:, :, P : 2 * P], tag="after_first_silu")
+        quantize(uq[2], u2_bf)
         project(2, 0)
-        project(3, 0)
-        interleave(nc.scalar.copy, cq[1])
         scatter(1, 0)
-        quantize(cq[1])
+        quantize(uq[3], u3_bf)
+        project(3, 0)
+        c1a_bf = interleave(on_scalar, "c1a_bf", c_raw[1][:, :, 0:P])
+        c1b_bf = interleave(on_scalar, "c1b_bf", c_raw[1][:, :, P : 2 * P])
+        scatter(2, 0)
+        quantize(xg[1], xg1a_bf)
+        quantize(xg[1], xg1b_bf, P)
+        quantize(cq[1], c1a_bf)
+        quantize(cq[1], c1b_bf, P)
         for t in range(M // P):
             project(t, 1)
-        scatter(2, 0)
         scatter(3, 0)
         for t in range(M // P):
             scatter(t, 1)

@@ -45,7 +45,7 @@ def tile_list_hboth_d_silu_kernel(tc, xT, w4_words, w4_scales, c, u, wgt, b, wgo
         warm_out = sb.tile([P, 8], F32, name="warm_out")
 
         def raw_tile(name, width):
-            return sb.tile([P, PACK, width], F32, name=name + "_raw")
+            return sb.tile([P, PACK, width], F32, name=name, tag=name, align_bytes=64)
 
         def operand(name, width):
             return {
@@ -53,15 +53,20 @@ def tile_list_hboth_d_silu_kernel(tc, xT, w4_words, w4_scales, c, u, wgt, b, wgo
                 "scale": sb.tile([P, width], U8, name=name + "_scale", align_bytes=64),
             }
 
-        xg_raw = [raw_tile(f"xg{h}", HALF) for h in range(2)]
-        c_raw = [raw_tile(f"c{h}", HALF) for h in range(2)]
-        u0_raw = sb.tile([P, PACK, P], F32, name="u0_raw", tag="after_u0", align_bytes=64)
-        u1_raw = raw_tile("u1", P)
-        u23_raw = raw_tile("u23", 2 * P)
-        xg = [operand(f"xg{h}", HALF) for h in range(2)]
-        cq = [operand(f"c{h}", HALF) for h in range(2)]
-        uq = [operand(f"u{t}", P) for t in range(M // P)]
-        first_bias = sb.tile([P, 1], F32, name="first_bias", tag="after_first_silu", align_bytes=64)
+        xg_raw = [raw_tile(f"xg{h}_raw", HALF) for h in range(2)]
+        c_raw = [raw_tile(f"c{h}_raw", HALF) for h in range(2)]
+        u_raw = [raw_tile(f"u{t}_raw", P) for t in range(2)]
+        u23_raw = raw_tile("u23_raw", 2 * P)
+
+        def columns(op, at, width):
+            return {"codes": op["codes"][:, at : at + width], "scale": op["scale"][:, at : at + width]}
+
+        xg0, c0, u0, u1 = operand("xg0", HALF), operand("c0", HALF), operand("u0", P), operand("u1", P)
+        u23, xg1, c1 = operand("u23", 2 * P), operand("xg1", HALF), operand("c1", HALF)
+        xg = [columns(xg0, 0, HALF), columns(xg1, 0, HALF)]
+        cq = [columns(c0, 0, HALF), columns(c1, 0, HALF)]
+        uq = [columns(u0, 0, P), columns(u1, 0, P), columns(u23, 0, P), columns(u23, P, P)]
+        own_bias = [sb.tile([P, 1], F32, name=f"bias{t}", tag=f"bias{t}", align_bytes=64) for t in range(3)]
 
         x_rows = xT.rearrange("(p i) t -> p i t", i=PACK)
         c_rows = c.rearrange("(p i) j -> p i j", i=PACK)
@@ -76,29 +81,31 @@ def tile_list_hboth_d_silu_kernel(tc, xT, w4_words, w4_scales, c, u, wgt, b, wgo
         nc.gpsimd.memset(w4_scale[:].bitcast(I32), 0)
         nc.gpsimd.memset(bias_rows[:], 0.0)
         nc.gpsimd.memset(warm[:], 0.0)
-        for q in range(4):
-            nc.scalar.dma_start(w4_scale[32 * q : 32 * q + 4, :].bitcast(I32), w4_scales[0, 4 * q : 4 * q + 4, :].bitcast(I32))
-        nc.scalar.dma_start(bias_rows[0 : M // P, :], b.rearrange("(t p) -> t p", p=P))
         nc.scalar.activation(warm_out[:], warm[:], SILU)
         make_identity(nc, identity[:])
-        bias_ps = psum.tile([P, P], F32, name="acc3_1")
-        nc.tensor.transpose(bias_ps[:], bias_rows[:], identity[:])
-        nc.scalar.copy(bias[:], bias_ps[:, 0 : M // P])
-        nc.scalar.copy(first_bias[:], bias_ps[:, 0:1])
 
         nc.sync.dma_start(gather_list[:], offs)
         nc.sync.dma_start(wgt_sb[:], wgt)
-        for i in range(PACK):
+        for i in range(PACK - 1):
             nc.sync.dma_start(planes[i][:], x_rows[:, i, :])
+        nc.sync.dma_start(bias_rows[0 : M // P, :], b.rearrange("(t p) -> t p", p=P))
+        for q in range(4):
+            nc.sync.dma_start(w4_scale[32 * q : 32 * q + 4, :].bitcast(I32), w4_scales[0, 4 * q : 4 * q + 4, :].bitcast(I32))
+        nc.sync.dma_start(planes[PACK - 1][:], x_rows[:, PACK - 1, :])
         nc.sync.dma_start(c_raw[0][:], c_rows[:, :, half(0)])
-        nc.sync.dma_start(u0_raw[:], u_rows[:, :, 0:P])
+        nc.sync.dma_start(u_raw[0][:], u_rows[:, :, 0:P])
         nc.sync.dma_start(w4_sb[:].bitcast(I32), w4_words[0].bitcast(I32))
-        nc.sync.dma_start(u1_raw[:], u_rows[:, :, P : 2 * P])
+        nc.sync.dma_start(u_raw[1][:], u_rows[:, :, P : 2 * P])
         nc.sync.dma_start(scatter_list[:], offs2)
-        nc.sync.dma_start(wgo_sb[:, half(0)], wgo[:, half(0)])
+        nc.sync.dma_start(wgo_sb[:], wgo)
         nc.sync.dma_start(u23_raw[:], u_rows[:, :, 2 * P : 4 * P])
         nc.sync.dma_start(c_raw[1][:], c_rows[:, :, half(1)])
-        nc.sync.dma_start(wgo_sb[:, half(1)], wgo[:, half(1)])
+
+        bias_ps = psum.tile([P, P], F32, name="bias_ps", tag="acc3_1")
+        nc.tensor.transpose(bias_ps[:], bias_rows[:], identity[:])
+        nc.scalar.copy(bias[:], bias_ps[:, 0 : M // P])
+        for t, column in enumerate(own_bias):
+            nc.scalar.copy(column[:], bias_ps[:, t : t + 1])
 
         for window in windows[:2]:
             nc.vector.memset(window[:], 0.0)
@@ -108,43 +115,58 @@ def tile_list_hboth_d_silu_kernel(tc, xT, w4_words, w4_scales, c, u, wgt, b, wgo
         def gather(i, h):
             nc.vector.tensor_tensor(xg_raw[h][:, i, :], planes[i][:].indirect(gather_list[:, list_half(h)]), wgt_sb[:, half(h)], MULT)
 
-        def interleave(copy, name, raw, tag=None):
-            width = raw.shape[2]
-            grouped = sb.tile([P, width, PACK], BF16, name=name, tag=tag or name, align_bytes=64)
-            copy(grouped[:].rearrange("p (c r) i -> p c i r", r=4), raw.rearrange("p i (c r) -> p c i r", r=4))
-            return grouped
+        def bf16_tile(name, width, tag=None):
+            return sb.tile([P, width, PACK], BF16, name=name, tag=tag or name, align_bytes=64)
 
-        def quantize(op, grouped, at=0):
-            cols = slice(at, at + grouped.shape[1])
-            nc.vector.quantize_mx(out=op["codes"][:, cols].bitcast(FP8X4), scales=op["scale"][:, cols], in_=grouped[:].rearrange("p w i -> p (w i)"))
+        def interleave(copy, grouped, raw):
+            copy(grouped.rearrange("p (c r) i -> p c i r", r=4), raw.rearrange("p i (c r) -> p c i r", r=4))
+
+        def quantize(op, grouped):
+            nc.vector.quantize_mx(out=op["codes"][:].bitcast(FP8X4), scales=op["scale"][:], in_=grouped[:].rearrange("p w i -> p (w i)"))
+
+        def w4_pass(acc, t, h, cols):
+            nc.tensor.matmul_mx(
+                out=acc,
+                lhsT=w4_sb[:, 2 * P * t : 2 * P * (t + 1)].bitcast(FP4X4),
+                lhsT_scale=w4_scale[:, P * t : P * (t + 1)],
+                rhs=xg[h]["codes"][:, cols].bitcast(FP8X4),
+                rhs_scale=xg[h]["scale"][:, cols],
+                start=True,
+                stop=False,
+            )
+
+        def u_pass(acc, t, h, cols):
+            nc.tensor.matmul_mx(
+                out=acc,
+                lhsT=uq[t]["codes"].bitcast(FP8X4),
+                lhsT_scale=uq[t]["scale"],
+                rhs=cq[h]["codes"][:, cols].bitcast(FP8X4),
+                rhs_scale=cq[h]["scale"][:, cols],
+                start=False,
+                stop=True,
+            )
 
         acts = {}
+        quarters = [slice(0, N_PASS), slice(N_PASS, HALF)]
 
-        def project(t, h):
-            acc = psum.tile([P, HALF], F32, name=f"acc{t}_{h}")
-            for j0 in range(0, HALF, N_PASS):
-                cols = slice(j0, j0 + N_PASS)
-                nc.tensor.matmul_mx(
-                    out=acc[:, cols],
-                    lhsT=w4_sb[:, 2 * P * t : 2 * P * (t + 1)].bitcast(FP4X4),
-                    lhsT_scale=w4_scale[:, P * t : P * (t + 1)],
-                    rhs=xg[h]["codes"][:, cols].bitcast(FP8X4),
-                    rhs_scale=xg[h]["scale"][:, cols],
-                    start=True,
-                    stop=False,
-                )
-                nc.tensor.matmul_mx(
-                    out=acc[:, cols],
-                    lhsT=uq[t]["codes"][:].bitcast(FP8X4),
-                    lhsT_scale=uq[t]["scale"][:],
-                    rhs=cq[h]["codes"][:, cols].bitcast(FP8X4),
-                    rhs_scale=cq[h]["scale"][:, cols],
-                    start=False,
-                    stop=True,
-                )
-            act = sb.tile([P, HALF], F32, name=f"act{t}_{h}")
-            nc.scalar.activation(act[:], acc[:], SILU, bias=first_bias[:] if (t, h) == (0, 0) else bias[:, t : t + 1])
+        def project(t, h, tag=None):
+            acc = psum.tile([P, HALF], F32, name=f"acc{t}_{h}", tag=f"acc{t}_{h}")
+            for cols in quarters:
+                w4_pass(acc[:, cols], t, h, cols)
+                u_pass(acc[:, cols], t, h, cols)
+            act = sb.tile([P, HALF], F32, name=f"act{t}_{h}", tag=tag or f"act{t}_{h}", align_bytes=64)
+            nc.scalar.activation(act[:], acc[:], SILU, bias=own_bias[t][:] if h == 0 and t < 3 else bias[:, t : t + 1])
             acts.setdefault((t, h), act)
+
+        def project_first():
+            accs = [psum.tile([P, N_PASS], F32, name=f"first{n}", tag=tag) for n, tag in enumerate(("acc0_0", "acc3_1"))]
+            for acc, cols in zip(accs, quarters):
+                w4_pass(acc[:], 0, 0, cols)
+            act = sb.tile([P, HALF], F32, name="act0_0")
+            for acc, cols in zip(accs, quarters):
+                u_pass(acc[:], 0, 0, cols)
+                nc.scalar.activation(act[:, cols], acc[:], SILU, bias=own_bias[0][:])
+            acts.setdefault((0, 0), act)
 
         def scatter(t, h):
             nc.vector.tensor_tensor(windows[t][:].indirect(scatter_list[:, list_half(h)]), acts[(t, h)][:], wgo_sb[:, half(h)], MULT)
@@ -154,37 +176,39 @@ def tile_list_hboth_d_silu_kernel(tc, xT, w4_words, w4_scales, c, u, wgt, b, wgo
             gather(i, 0)
             gather(i, 1)
         gather(3, 0)
-        xg0_bf = interleave(on_scalar, "xg0_bf", xg_raw[0][:])
+        xg0_bf = bf16_tile("xg0_bf", HALF)
+        interleave(on_vector, xg0_bf[:, 0:P, :], xg_raw[0][:, :, 0:P])
+        interleave(on_scalar, xg0_bf[:, P:HALF, :], xg_raw[0][:, :, P:HALF])
+        c0_bf = bf16_tile("c0_bf", HALF)
+        interleave(on_vector, c0_bf[:], c_raw[0][:])
+        u0_bf = xg_raw[1][:, PACK - 1, :].bitcast(BF16).rearrange("p (w i) -> p w i", i=PACK)
+        interleave(on_scalar, u0_bf, u_raw[0][:])
+        quantize(xg0, xg0_bf)
+        quantize(c0, c0_bf)
+        quantize(u0, u0_bf)
+        project_first()
+        u1_bf = bf16_tile("u1_bf", P, tag="c0_bf")
+        interleave(on_vector, u1_bf[:], u_raw[1][:])
         gather(3, 1)
-        c0_bf = interleave(on_vector, "c0_bf", c_raw[0][:])
-        u0_bf = interleave(on_scalar, "u0_bf", u0_raw[:])
-        quantize(xg[0], xg0_bf)
-        quantize(cq[0], c0_bf)
-        quantize(uq[0], u0_bf)
-        project(0, 0)
-        u1_bf = interleave(on_vector, "u1_bf", u1_raw[:])
-        quantize(uq[1], u1_bf)
-        project(1, 0)
+        quantize(u1, u1_bf)
         scatter(0, 0)
-        u2_bf = interleave(on_scalar, "u2_bf", u23_raw[:, :, 0:P])
-        u3_bf = interleave(on_scalar, "u3_bf", u23_raw[:, :, P : 2 * P])
-        xg1a_bf = interleave(on_scalar, "xg1a_bf", xg_raw[1][:, :, 0:P], tag="after_u0")
-        xg1b_bf = interleave(on_scalar, "xg1b_bf", xg_raw[1][:, :, P : 2 * P], tag="after_first_silu")
-        quantize(uq[2], u2_bf)
-        project(2, 0)
+        u23_bf = bf16_tile("u23_bf", 2 * P, tag="bias0")
+        interleave(on_scalar, u23_bf[:], u23_raw[:])
+        project(1, 0, tag="u23_raw")
+        quantize(u23, u23_bf)
         scatter(1, 0)
-        quantize(uq[3], u3_bf)
-        project(3, 0)
-        c1a_bf = interleave(on_scalar, "c1a_bf", c_raw[1][:, :, 0:P])
-        c1b_bf = interleave(on_scalar, "c1b_bf", c_raw[1][:, :, P : 2 * P])
+        xg1_bf = bf16_tile("xg1_bf", HALF, tag="bias1")
+        interleave(on_scalar, xg1_bf[:], xg_raw[1][:])
+        project(2, 0, tag="xg1_raw")
+        quantize(xg1, xg1_bf)
         scatter(2, 0)
-        quantize(xg[1], xg1a_bf)
-        quantize(xg[1], xg1b_bf, P)
-        quantize(cq[1], c1a_bf)
-        quantize(cq[1], c1b_bf, P)
+        c1_bf = bf16_tile("c1_bf", HALF, tag="bias2")
+        interleave(on_scalar, c1_bf[:], c_raw[1][:])
+        project(3, 0, tag="c1_raw")
+        quantize(c1, c1_bf)
+        scatter(3, 0)
         for t in range(M // P):
             project(t, 1)
-        scatter(3, 0)
         for t in range(M // P):
             scatter(t, 1)
             nc.sync.dma_start(out[P * t : P * (t + 1), :], windows[t][:])

@@ -107,9 +107,9 @@ def tile_list_hboth_d_silu_kernel(tc, xT, w4_words, w4_scales, c, u, wgt, b, wgo
         for t, column in enumerate(own_bias):
             nc.scalar.copy(column[:], bias_ps[:, t : t + 1])
 
-        for window in windows[:2]:
+        for window in windows[:3]:
             nc.vector.memset(window[:], 0.0)
-        for window in windows[2:]:
+        for window in windows[3:]:
             nc.gpsimd.memset(window[:], 0.0)
 
         def gather(i, h):

@@ -21,7 +21,6 @@ P = 128
 PACK = 4
 HALF = S // 2
 N_PASS = 128
-LIST_COLS = HALF // 16
 
 
 def tile_list_hboth_d_silu_kernel(tc, xT, w4_words, w4_scales, c, u, wgt, b, wgo, offs, offs2, out):
@@ -53,20 +52,14 @@ def tile_list_hboth_d_silu_kernel(tc, xT, w4_words, w4_scales, c, u, wgt, b, wgo
                 "scale": sb.tile([P, width], U8, name=name + "_scale", align_bytes=64),
             }
 
-        xg_raw = [raw_tile(f"xg{h}_raw", HALF) for h in range(2)]
+        def columns(op, cols):
+            return {"codes": op["codes"][:, cols], "scale": op["scale"][:, cols]}
+
+        xg_raw = raw_tile("xg_raw", S)
         c_raw = [raw_tile(f"c{h}_raw", HALF) for h in range(2)]
-        u_raw = [raw_tile(f"u{t}_raw", P) for t in range(2)]
-        u23_raw = raw_tile("u23_raw", 2 * P)
-
-        def columns(op, at, width):
-            return {"codes": op["codes"][:, at : at + width], "scale": op["scale"][:, at : at + width]}
-
-        xg0, c0, u0, u1 = operand("xg0", HALF), operand("c0", HALF), operand("u0", P), operand("u1", P)
-        u23, xg1, c1 = operand("u23", 2 * P), operand("xg1", HALF), operand("c1", HALF)
-        xg = [columns(xg0, 0, HALF), columns(xg1, 0, HALF)]
-        cq = [columns(c0, 0, HALF), columns(c1, 0, HALF)]
-        uq = [columns(u0, 0, P), columns(u1, 0, P), columns(u23, 0, P), columns(u23, P, P)]
-        own_bias = [sb.tile([P, 1], F32, name=f"bias{t}", tag=f"bias{t}", align_bytes=64) for t in range(3)]
+        u_raw = [raw_tile(f"u{h}_raw", HALF) for h in range(2)]
+        xg, cq, uq = operand("xg", S), operand("cq", S), operand("uq", M)
+        held_bias = [sb.tile([P, 1], F32, name=f"held_bias{n}", tag=f"held_bias{n}", align_bytes=64) for n in range(4)]
 
         x_rows = xT.rearrange("(p i) t -> p i t", i=PACK)
         c_rows = c.rearrange("(p i) j -> p i j", i=PACK)
@@ -75,8 +68,16 @@ def tile_list_hboth_d_silu_kernel(tc, xT, w4_words, w4_scales, c, u, wgt, b, wgo
         def half(h):
             return slice(h * HALF, (h + 1) * HALF)
 
-        def list_half(h):
-            return slice(h * LIST_COLS, (h + 1) * LIST_COLS)
+        def rows(t):
+            return slice(P * t, P * (t + 1))
+
+        def listed(cols):
+            return slice(cols.start // 16, cols.stop // 16)
+
+        def quarter(q):
+            return slice(q * N_PASS, (q + 1) * N_PASS)
+
+        whole = slice(0, S)
 
         nc.gpsimd.memset(w4_scale[:].bitcast(I32), 0)
         nc.gpsimd.memset(bias_rows[:], 0.0)
@@ -92,19 +93,19 @@ def tile_list_hboth_d_silu_kernel(tc, xT, w4_words, w4_scales, c, u, wgt, b, wgo
         for q in range(4):
             nc.sync.dma_start(w4_scale[32 * q : 32 * q + 4, :].bitcast(I32), w4_scales[0, 4 * q : 4 * q + 4, :].bitcast(I32))
         nc.sync.dma_start(planes[PACK - 1][:], x_rows[:, PACK - 1, :])
+        nc.sync.dma_start(u_raw[0][:], u_rows[:, :, half(0)])
         nc.sync.dma_start(c_raw[0][:], c_rows[:, :, half(0)])
-        nc.sync.dma_start(u_raw[0][:], u_rows[:, :, 0:P])
         nc.sync.dma_start(w4_sb[:].bitcast(I32), w4_words[0].bitcast(I32))
-        nc.sync.dma_start(u_raw[1][:], u_rows[:, :, P : 2 * P])
         nc.sync.dma_start(scatter_list[:], offs2)
-        nc.sync.dma_start(wgo_sb[:], wgo)
-        nc.sync.dma_start(u23_raw[:], u_rows[:, :, 2 * P : 4 * P])
+        nc.sync.dma_start(wgo_sb[:, half(0)], wgo[:, half(0)])
         nc.sync.dma_start(c_raw[1][:], c_rows[:, :, half(1)])
+        nc.sync.dma_start(wgo_sb[:, half(1)], wgo[:, half(1)])
+        nc.sync.dma_start(u_raw[1][:], u_rows[:, :, half(1)])
 
-        bias_ps = psum.tile([P, P], F32, name="bias_ps", tag="acc3_1")
+        bias_ps = psum.tile([P, P], F32, name="bias_ps", tag="bias_ps")
         nc.tensor.transpose(bias_ps[:], bias_rows[:], identity[:])
         nc.scalar.copy(bias[:], bias_ps[:, 0 : M // P])
-        for t, column in enumerate(own_bias):
+        for column, t in zip(held_bias, (1, 0, 1, 0)):
             nc.scalar.copy(column[:], bias_ps[:, t : t + 1])
 
         for window in windows[:3]:
@@ -112,8 +113,8 @@ def tile_list_hboth_d_silu_kernel(tc, xT, w4_words, w4_scales, c, u, wgt, b, wgo
         for window in windows[3:]:
             nc.gpsimd.memset(window[:], 0.0)
 
-        def gather(i, h):
-            nc.vector.tensor_tensor(xg_raw[h][:, i, :], planes[i][:].indirect(gather_list[:, list_half(h)]), wgt_sb[:, half(h)], MULT)
+        def gather(i, cols):
+            nc.vector.tensor_tensor(xg_raw[:, i, cols], planes[i][:].indirect(gather_list[:, listed(cols)]), wgt_sb[:, cols], MULT)
 
         def bf16_tile(name, width, tag=None):
             return sb.tile([P, width, PACK], BF16, name=name, tag=tag or name, align_bytes=64)
@@ -122,93 +123,94 @@ def tile_list_hboth_d_silu_kernel(tc, xT, w4_words, w4_scales, c, u, wgt, b, wgo
             copy(grouped.rearrange("p (c r) i -> p c i r", r=4), raw.rearrange("p i (c r) -> p c i r", r=4))
 
         def quantize(op, grouped):
-            nc.vector.quantize_mx(out=op["codes"][:].bitcast(FP8X4), scales=op["scale"][:], in_=grouped[:].rearrange("p w i -> p (w i)"))
+            nc.vector.quantize_mx(out=op["codes"].bitcast(FP8X4), scales=op["scale"], in_=grouped.rearrange("p w i -> p (w i)"))
 
-        def w4_pass(acc, t, h, cols):
+        def w4_pass(acc, t, cols, start, stop):
             nc.tensor.matmul_mx(
                 out=acc,
                 lhsT=w4_sb[:, 2 * P * t : 2 * P * (t + 1)].bitcast(FP4X4),
-                lhsT_scale=w4_scale[:, P * t : P * (t + 1)],
-                rhs=xg[h]["codes"][:, cols].bitcast(FP8X4),
-                rhs_scale=xg[h]["scale"][:, cols],
-                start=True,
-                stop=False,
+                lhsT_scale=w4_scale[:, rows(t)],
+                rhs=xg["codes"][:, cols].bitcast(FP8X4),
+                rhs_scale=xg["scale"][:, cols],
+                start=start,
+                stop=stop,
             )
 
-        def u_pass(acc, t, h, cols):
+        def u_pass(acc, t, cols, start, stop):
             nc.tensor.matmul_mx(
                 out=acc,
-                lhsT=uq[t]["codes"].bitcast(FP8X4),
-                lhsT_scale=uq[t]["scale"],
-                rhs=cq[h]["codes"][:, cols].bitcast(FP8X4),
-                rhs_scale=cq[h]["scale"][:, cols],
-                start=False,
-                stop=True,
+                lhsT=uq["codes"][:, rows(t)].bitcast(FP8X4),
+                lhsT_scale=uq["scale"][:, rows(t)],
+                rhs=cq["codes"][:, cols].bitcast(FP8X4),
+                rhs_scale=cq["scale"][:, cols],
+                start=start,
+                stop=stop,
             )
 
-        acts = {}
-        quarters = [slice(0, N_PASS), slice(N_PASS, HALF)]
+        def project(t, cols, bank, bias_column, w4_first, tag=None):
+            width = cols.stop - cols.start
+            step = N_PASS if width < S else S
+            acc = psum.tile([P, width], F32, name=f"acc{t}_{cols.start}", tag=bank)
+            if not w4_first:
+                u_pass(acc[:], t, cols, True, False)
+            for at in range(0, width, step):
+                w4_pass(acc[:, at : at + step], t, slice(cols.start + at, cols.start + at + step), w4_first and at == 0, not w4_first and at + step == width)
+            if w4_first:
+                u_pass(acc[:], t, cols, False, True)
+            name = f"act{t}_{cols.start}"
+            act = sb.tile([P, width], F32, name=name, tag=tag or name, align_bytes=64)
+            nc.scalar.activation(act[:], acc[:], SILU, bias=bias_column)
+            return act
 
-        def project(t, h, tag=None):
-            acc = psum.tile([P, HALF], F32, name=f"acc{t}_{h}", tag=f"acc{t}_{h}")
-            for cols in quarters:
-                w4_pass(acc[:, cols], t, h, cols)
-                u_pass(acc[:, cols], t, h, cols)
-            act = sb.tile([P, HALF], F32, name=f"act{t}_{h}", tag=tag or f"act{t}_{h}", align_bytes=64)
-            nc.scalar.activation(act[:], acc[:], SILU, bias=own_bias[t][:] if h == 0 and t < 3 else bias[:, t : t + 1])
-            acts.setdefault((t, h), act)
+        def scatter(t, cols, act):
+            nc.vector.tensor_tensor(windows[t][:].indirect(scatter_list[:, listed(cols)]), act[:], wgo_sb[:, cols], MULT)
 
-        def project_first():
-            accs = [psum.tile([P, N_PASS], F32, name=f"first{n}", tag=tag) for n, tag in enumerate(("acc0_0", "acc3_1"))]
-            for acc, cols in zip(accs, quarters):
-                w4_pass(acc[:], 0, 0, cols)
-            act = sb.tile([P, HALF], F32, name="act0_0")
-            for acc, cols in zip(accs, quarters):
-                u_pass(acc[:], 0, 0, cols)
-                nc.scalar.activation(act[:, cols], acc[:], SILU, bias=own_bias[0][:])
-            acts.setdefault((0, 0), act)
-
-        def scatter(t, h):
-            nc.vector.tensor_tensor(windows[t][:].indirect(scatter_list[:, list_half(h)]), acts[(t, h)][:], wgo_sb[:, half(h)], MULT)
+        def store(t):
+            nc.sync.dma_start(out[rows(t), :], windows[t][:])
 
         on_scalar, on_vector = nc.scalar.copy, nc.vector.tensor_copy
         for i in range(PACK - 1):
-            gather(i, 0)
-            gather(i, 1)
-        gather(3, 0)
-        xg0_bf = bf16_tile("xg0_bf", HALF)
-        interleave(on_vector, xg0_bf[:, 0:P, :], xg_raw[0][:, :, 0:P])
-        interleave(on_scalar, xg0_bf[:, P:HALF, :], xg_raw[0][:, :, P:HALF])
-        c0_bf = bf16_tile("c0_bf", HALF)
-        interleave(on_vector, c0_bf[:], c_raw[0][:])
-        u0_bf = xg_raw[1][:, PACK - 1, :].bitcast(BF16).rearrange("p (w i) -> p w i", i=PACK)
-        interleave(on_scalar, u0_bf, u_raw[0][:])
-        quantize(xg0, xg0_bf)
-        quantize(c0, c0_bf)
-        quantize(u0, u0_bf)
-        project_first()
-        u1_bf = bf16_tile("u1_bf", P, tag="c0_bf")
-        interleave(on_vector, u1_bf[:], u_raw[1][:])
-        gather(3, 1)
-        quantize(u1, u1_bf)
-        scatter(0, 0)
-        u23_bf = bf16_tile("u23_bf", 2 * P, tag="bias0")
-        interleave(on_scalar, u23_bf[:], u23_raw[:])
-        project(1, 0, tag="u23_raw")
-        quantize(u23, u23_bf)
-        scatter(1, 0)
-        xg1_bf = bf16_tile("xg1_bf", HALF, tag="bias1")
-        interleave(on_scalar, xg1_bf[:], xg_raw[1][:])
-        project(2, 0, tag="xg1_raw")
-        quantize(xg1, xg1_bf)
-        scatter(2, 0)
-        c1_bf = bf16_tile("c1_bf", HALF, tag="bias2")
+            gather(i, whole)
+        for cols in (quarter(0), quarter(1), half(1)):
+            gather(PACK - 1, cols)
+        xg_bf = [bf16_tile(f"xg{q}_bf", N_PASS) for q in range(2)]
+        u_bf = [bf16_tile(f"u{t}_bf", P) for t in range(2)]
+        c_bf = [bf16_tile(f"c{q}_bf", N_PASS) for q in range(2)]
+        interleave(on_scalar, xg_bf[0][:], xg_raw[:, :, quarter(0)])
+        interleave(on_vector, xg_bf[1][:], xg_raw[:, :, quarter(1)])
+        for t in range(2):
+            interleave(on_scalar, u_bf[t][:], u_raw[0][:, :, rows(t)])
+        for q in range(2):
+            quantize(columns(xg, quarter(q)), xg_bf[q][:])
+        quantize(columns(uq, rows(0)), u_bf[0][:])
+        interleave(on_vector, c_bf[0][:], c_raw[0][:, :, quarter(0)])
+        interleave(on_scalar, c_bf[1][:], c_raw[0][:, :, quarter(1)])
+        quantize(columns(uq, rows(1)), u_bf[1][:])
+        quantize(columns(cq, quarter(0)), c_bf[0][:])
+        act0 = project(0, quarter(0), "bank0", bias[:, 0:1], True)
+        act1 = project(1, quarter(0), "bank1", held_bias[0][:], True)
+        xg_late_bf = bf16_tile("xg_late_bf", HALF, tag="c0_raw")
+        interleave(on_vector, xg_late_bf[:], xg_raw[:, :, half(1)])
+        quantize(columns(cq, quarter(1)), c_bf[1][:])
+        quantize(columns(xg, half(1)), xg_late_bf[:])
+        scatter(0, quarter(0), act0)
+        scatter(1, quarter(0), act1)
+        c1_bf = bf16_tile("c_late_bf", HALF, tag="held_bias0")
         interleave(on_scalar, c1_bf[:], c_raw[1][:])
-        project(3, 0, tag="c1_raw")
-        quantize(c1, c1_bf)
-        scatter(3, 0)
-        for t in range(M // P):
-            project(t, 1)
-        for t in range(M // P):
-            scatter(t, 1)
-            nc.sync.dma_start(out[P * t : P * (t + 1), :], windows[t][:])
+        act0 = project(0, quarter(1), "bank2", held_bias[1][:], False, tag="c1_raw")
+        act1 = project(1, quarter(1), "bank3", held_bias[2][:], False, tag="held_bias1")
+        quantize(columns(cq, half(1)), c1_bf[:])
+        scatter(0, quarter(1), act0)
+        scatter(1, quarter(1), act1)
+        u23_bf = bf16_tile("u23_bf", HALF, tag="held_bias2")
+        interleave(on_scalar, u23_bf[:], u_raw[1][:])
+        act0 = project(0, half(1), "bank0", held_bias[3][:], True, tag="u1_raw")
+        act1 = project(1, half(1), "bank1", bias[:, 1:2], True, tag="held_bias3")
+        quantize(columns(uq, half(1)), u23_bf[:])
+        for t, act in enumerate((act0, act1)):
+            scatter(t, half(1), act)
+            store(t)
+        for t in range(2, M // P):
+            act = project(t, whole, f"bank{t}", bias[:, t : t + 1], True)
+            scatter(t, whole, act)
+            store(t)

@@ -59,7 +59,7 @@ def tile_list_hboth_d_silu_kernel(tc, xT, w4_words, w4_scales, c, u, wgt, b, wgo
         c_raw = [raw_tile(f"c{h}_raw", HALF) for h in range(2)]
         u_raw = [raw_tile(f"u{h}_raw", HALF) for h in range(2)]
         xg, cq, uq = operand("xg", S), operand("cq", S), operand("uq", M)
-        held_bias = [sb.tile([P, 1], F32, name=f"held_bias{n}", tag=f"held_bias{n}", align_bytes=64) for n in range(4)]
+        held_bias = [sb.tile([P, 1], F32, name=f"held_bias{n}", tag=f"held_bias{n}", align_bytes=64) for n in range(3)]
 
         x_rows = xT.rearrange("(p i) t -> p i t", i=PACK)
         c_rows = c.rearrange("(p i) j -> p i j", i=PACK)
@@ -86,8 +86,10 @@ def tile_list_hboth_d_silu_kernel(tc, xT, w4_words, w4_scales, c, u, wgt, b, wgo
         make_identity(nc, identity[:])
 
         nc.sync.dma_start(gather_list[:], offs)
-        nc.sync.dma_start(wgt_sb[:], wgt)
-        for i in range(PACK - 1):
+        nc.sync.dma_start(wgt_sb[:, half(0)], wgt[:, half(0)])
+        nc.sync.dma_start(planes[0][:], x_rows[:, 0, :])
+        nc.sync.dma_start(wgt_sb[:, half(1)], wgt[:, half(1)])
+        for i in range(1, PACK - 1):
             nc.sync.dma_start(planes[i][:], x_rows[:, i, :])
         nc.sync.dma_start(bias_rows[0 : M // P, :], b.rearrange("(t p) -> t p", p=P))
         for q in range(4):
@@ -105,12 +107,12 @@ def tile_list_hboth_d_silu_kernel(tc, xT, w4_words, w4_scales, c, u, wgt, b, wgo
         bias_ps = psum.tile([P, P], F32, name="bias_ps", tag="bias_ps")
         nc.tensor.transpose(bias_ps[:], bias_rows[:], identity[:])
         nc.scalar.copy(bias[:], bias_ps[:, 0 : M // P])
-        for column, t in zip(held_bias, (1, 0, 1, 0)):
+        for column, t in zip(held_bias, (1, 0, 0)):
             nc.scalar.copy(column[:], bias_ps[:, t : t + 1])
 
-        for window in windows[:3]:
+        for window in windows[:2]:
             nc.vector.memset(window[:], 0.0)
-        for window in windows[3:]:
+        for window in windows[2:]:
             nc.gpsimd.memset(window[:], 0.0)
 
         def gather(i, cols):
@@ -169,7 +171,9 @@ def tile_list_hboth_d_silu_kernel(tc, xT, w4_words, w4_scales, c, u, wgt, b, wgo
             nc.sync.dma_start(out[rows(t), :], windows[t][:])
 
         on_scalar, on_vector = nc.scalar.copy, nc.vector.tensor_copy
-        for i in range(PACK - 1):
+        for h in range(2):
+            gather(0, half(h))
+        for i in range(1, PACK - 1):
             gather(i, whole)
         for cols in (quarter(0), quarter(1), half(1)):
             gather(PACK - 1, cols)
@@ -189,8 +193,9 @@ def tile_list_hboth_d_silu_kernel(tc, xT, w4_words, w4_scales, c, u, wgt, b, wgo
         quantize(columns(cq, quarter(0)), c_bf[0][:])
         act0 = project(0, quarter(0), "bank0", bias[:, 0:1], True)
         act1 = project(1, quarter(0), "bank1", held_bias[0][:], True)
-        xg_late_bf = bf16_tile("xg_late_bf", HALF, tag="c0_raw")
-        interleave(on_vector, xg_late_bf[:], xg_raw[:, :, half(1)])
+        xg_late_bf = bf16_tile("xg_late_bf", HALF, tag="u1_bf")
+        interleave(on_vector, xg_late_bf[:, 0:P, :], xg_raw[:, :, quarter(2)])
+        interleave(on_scalar, xg_late_bf[:, P:HALF, :], xg_raw[:, :, quarter(3)])
         quantize(columns(cq, quarter(1)), c_bf[1][:])
         quantize(columns(xg, half(1)), xg_late_bf[:])
         scatter(0, quarter(0), act0)
@@ -198,19 +203,24 @@ def tile_list_hboth_d_silu_kernel(tc, xT, w4_words, w4_scales, c, u, wgt, b, wgo
         c1_bf = bf16_tile("c_late_bf", HALF, tag="held_bias0")
         interleave(on_scalar, c1_bf[:], c_raw[1][:])
         act0 = project(0, quarter(1), "bank2", held_bias[1][:], False, tag="c1_raw")
-        act1 = project(1, quarter(1), "bank3", held_bias[2][:], False, tag="held_bias1")
+        act1 = project(1, quarter(1), "bank3", bias[:, 1:2], False, tag="held_bias1")
         quantize(columns(cq, half(1)), c1_bf[:])
         scatter(0, quarter(1), act0)
         scatter(1, quarter(1), act1)
+        act0 = project(0, half(1), "bank0", held_bias[2][:], True)
         u23_bf = bf16_tile("u23_bf", HALF, tag="held_bias2")
         interleave(on_scalar, u23_bf[:], u_raw[1][:])
-        act0 = project(0, half(1), "bank0", held_bias[3][:], True, tag="u1_raw")
-        act1 = project(1, half(1), "bank1", bias[:, 1:2], True, tag="held_bias3")
+        act1 = project(1, half(1), "bank1", bias[:, 1:2], True, tag="u1_raw")
+        scatter(0, half(1), act0)
+        store(0)
         quantize(columns(uq, half(1)), u23_bf[:])
-        for t, act in enumerate((act0, act1)):
-            scatter(t, half(1), act)
-            store(t)
-        for t in range(2, M // P):
-            act = project(t, whole, f"bank{t}", bias[:, t : t + 1], True)
-            scatter(t, whole, act)
-            store(t)
+        scatter(1, half(1), act1)
+        store(1)
+        act2 = project(2, half(0), "bank2", bias[:, 2:3], True)
+        act3 = project(3, whole, "bank3", bias[:, 3:4], True)
+        last = project(2, half(1), "bank4", bias[:, 2:3], False)
+        scatter(2, half(0), act2)
+        scatter(3, whole, act3)
+        store(3)
+        scatter(2, half(1), last)
+        store(2)

@@ -173,15 +173,17 @@ def tile_list_hboth_d_silu_kernel(tc, xT, w4_words, w4_scales, c, u, wgt, b, wgo
         on_scalar, on_vector = nc.scalar.copy, nc.vector.tensor_copy
         for h in range(2):
             gather(0, half(h))
-        for i in range(1, PACK - 1):
-            gather(i, whole)
+        gather(1, whole)
+        xg_bf = [bf16_tile(f"xg{q}_bf", N_PASS) for q in range(2)]
+        for q in range(2):
+            interleave(on_scalar, xg_bf[q][:, :, 0:2], xg_raw[:, 0:2, quarter(q)])
+        gather(2, whole)
         for cols in (quarter(0), quarter(1), half(1)):
             gather(PACK - 1, cols)
-        xg_bf = [bf16_tile(f"xg{q}_bf", N_PASS) for q in range(2)]
         u_bf = [bf16_tile(f"u{t}_bf", P) for t in range(2)]
         c_bf = [bf16_tile(f"c{q}_bf", N_PASS) for q in range(2)]
-        interleave(on_scalar, xg_bf[0][:], xg_raw[:, :, quarter(0)])
-        interleave(on_vector, xg_bf[1][:], xg_raw[:, :, quarter(1)])
+        interleave(on_scalar, xg_bf[0][:, :, 2:4], xg_raw[:, 2:4, quarter(0)])
+        interleave(on_vector, xg_bf[1][:, :, 2:4], xg_raw[:, 2:4, quarter(1)])
         for t in range(2):
             interleave(on_scalar, u_bf[t][:], u_raw[0][:, :, rows(t)])
         for q in range(2):

@@ -59,6 +59,7 @@ def tile_list_hboth_d_silu_kernel(tc, xT, w4_words, w4_scales, c, u, wgt, b, wgo
         c_raw = [raw_tile(f"c{h}_raw", HALF) for h in range(2)]
         u_raw = [raw_tile(f"u{h}_raw", HALF) for h in range(2)]
         xg, cq, uq = operand("xg", S), operand("cq", S), operand("uq", M)
+        xg_codes = {q: xg["codes"][:, q * N_PASS : (q + 1) * N_PASS] for q in (0, 3)}
         held_bias = [sb.tile([P, 1], F32, name=f"held_bias{n}", tag=f"held_bias{n}", align_bytes=64) for n in range(3)]
 
         x_rows = xT.rearrange("(p i) t -> p i t", i=PACK)
@@ -99,15 +100,15 @@ def tile_list_hboth_d_silu_kernel(tc, xT, w4_words, w4_scales, c, u, wgt, b, wgo
         nc.sync.dma_start(c_raw[0][:], c_rows[:, :, half(0)])
         nc.sync.dma_start(w4_sb[:].bitcast(I32), w4_words[0].bitcast(I32))
         nc.sync.dma_start(scatter_list[:], offs2)
-        nc.sync.dma_start(wgo_sb[:, half(0)], wgo[:, half(0)])
+        nc.sync.dma_start(wgo_sb[:, quarter(0)], wgo[:, quarter(0)])
         nc.sync.dma_start(c_raw[1][:], c_rows[:, :, half(1)])
-        nc.sync.dma_start(wgo_sb[:, half(1)], wgo[:, half(1)])
+        nc.sync.dma_start(wgo_sb[:, N_PASS:S], wgo[:, N_PASS:S])
         nc.sync.dma_start(u_raw[1][:], u_rows[:, :, half(1)])
 
         bias_ps = psum.tile([P, P], F32, name="bias_ps", tag="bias_ps")
         nc.tensor.transpose(bias_ps[:], bias_rows[:], identity[:])
         nc.scalar.copy(bias[:], bias_ps[:, 0 : M // P])
-        for column, t in zip(held_bias, (1, 0, 0)):
+        for column, t in zip(held_bias, (0, 0, 0)):
             nc.scalar.copy(column[:], bias_ps[:, t : t + 1])
 
         for window in windows[:2]:
@@ -132,7 +133,7 @@ def tile_list_hboth_d_silu_kernel(tc, xT, w4_words, w4_scales, c, u, wgt, b, wgo
                 out=acc,
                 lhsT=w4_sb[:, 2 * P * t : 2 * P * (t + 1)].bitcast(FP4X4),
                 lhsT_scale=w4_scale[:, rows(t)],
-                rhs=xg["codes"][:, cols].bitcast(FP8X4),
+                rhs=xg_codes[cols.start // N_PASS].bitcast(FP8X4),
                 rhs_scale=xg["scale"][:, cols],
                 start=start,
                 stop=stop,
@@ -151,7 +152,7 @@ def tile_list_hboth_d_silu_kernel(tc, xT, w4_words, w4_scales, c, u, wgt, b, wgo
 
         def project(t, cols, bank, bias_column, w4_first, tag=None):
             width = cols.stop - cols.start
-            step = N_PASS if width < S else S
+            step = N_PASS
             acc = psum.tile([P, width], F32, name=f"acc{t}_{cols.start}", tag=bank)
             if not w4_first:
                 u_pass(acc[:], t, cols, True, False)
@@ -174,32 +175,35 @@ def tile_list_hboth_d_silu_kernel(tc, xT, w4_words, w4_scales, c, u, wgt, b, wgo
         for h in range(2):
             gather(0, half(h))
         gather(1, whole)
-        xg_bf = [bf16_tile(f"xg{q}_bf", N_PASS) for q in range(2)]
-        for q in range(2):
-            interleave(on_scalar, xg_bf[q][:, :, 0:2], xg_raw[:, 0:2, quarter(q)])
+        middle = slice(N_PASS, 3 * N_PASS)
+        xg_bf = [bf16_tile("xg0_bf", N_PASS), bf16_tile("xg12_bf", HALF)]
+        interleave(on_scalar, xg_bf[0][:, :, 0:2], xg_raw[:, 0:2, quarter(0)])
+        interleave(on_scalar, xg_bf[1][:, :, 0:2], xg_raw[:, 0:2, middle])
         gather(2, whole)
-        for cols in (quarter(0), quarter(1), half(1)):
+        for cols in (quarter(0), middle, quarter(3)):
             gather(PACK - 1, cols)
         u_bf = [bf16_tile(f"u{t}_bf", P) for t in range(2)]
         c_bf = [bf16_tile(f"c{q}_bf", N_PASS) for q in range(2)]
         interleave(on_scalar, xg_bf[0][:, :, 2:4], xg_raw[:, 2:4, quarter(0)])
-        interleave(on_vector, xg_bf[1][:, :, 2:4], xg_raw[:, 2:4, quarter(1)])
+        interleave(on_vector, xg_bf[1][:, :, 2:4], xg_raw[:, 2:4, middle])
         for t in range(2):
             interleave(on_scalar, u_bf[t][:], u_raw[0][:, :, rows(t)])
-        for q in range(2):
-            quantize(columns(xg, quarter(q)), xg_bf[q][:])
+        quantize(columns(xg, quarter(0)), xg_bf[0][:])
         quantize(columns(uq, rows(0)), u_bf[0][:])
         interleave(on_vector, c_bf[0][:], c_raw[0][:, :, quarter(0)])
         interleave(on_scalar, c_bf[1][:], c_raw[0][:, :, quarter(1)])
         quantize(columns(uq, rows(1)), u_bf[1][:])
         quantize(columns(cq, quarter(0)), c_bf[0][:])
-        act0 = project(0, quarter(0), "bank0", bias[:, 0:1], True)
-        act1 = project(1, quarter(0), "bank1", held_bias[0][:], True)
-        xg_late_bf = bf16_tile("xg_late_bf", HALF, tag="u1_bf")
-        interleave(on_vector, xg_late_bf[:, 0:P, :], xg_raw[:, :, quarter(2)])
-        interleave(on_scalar, xg_late_bf[:, P:HALF, :], xg_raw[:, :, quarter(3)])
+        act0 = project(0, quarter(0), "bank0", held_bias[0][:], True)
+        act1 = project(1, quarter(0), "bank1", bias[:, 1:2], True)
+        xg_late_bf = bf16_tile("xg_late_bf", N_PASS, tag="u1_bf")
+        interleave(on_vector, xg_late_bf[:, 0:64, :], xg_raw[:, :, 3 * N_PASS : 3 * N_PASS + 64])
+        interleave(on_scalar, xg_late_bf[:, 64:P, :], xg_raw[:, :, 3 * N_PASS + 64 : S])
+        middle_codes = sb.tile([P, HALF], U32, name="middle_codes", tag="c0_bf", align_bytes=64)
+        xg_codes[1], xg_codes[2] = middle_codes[:, quarter(0)], middle_codes[:, quarter(1)]
         quantize(columns(cq, quarter(1)), c_bf[1][:])
-        quantize(columns(xg, half(1)), xg_late_bf[:])
+        quantize({"codes": middle_codes[:], "scale": xg["scale"][:, middle]}, xg_bf[1][:])
+        quantize(columns(xg, quarter(3)), xg_late_bf[:])
         scatter(0, quarter(0), act0)
         scatter(1, quarter(0), act1)
         c1_bf = bf16_tile("c_late_bf", HALF, tag="held_bias0")

@@ -19,8 +19,13 @@ SILU = mybir.ActivationFunctionType.Silu
 
 P = 128
 PACK = 4
+ROW_TILES = M // P
 HALF = S // 2
-N_PASS = 128
+QUARTER = S // 4
+GROUP = 16
+RUN = 4
+MX_ALIGN = 64
+LAST_ON_VECTOR = QUARTER // 2
 
 
 def tile_list_hboth_d_silu_kernel(tc, xT, w4_words, w4_scales, c, u, wgt, b, wgo, offs, offs2, out):
@@ -29,56 +34,54 @@ def tile_list_hboth_d_silu_kernel(tc, xT, w4_words, w4_scales, c, u, wgt, b, wgo
         sb = ctx.enter_context(tc.tile_pool(name="sb", bufs=1))
         psum = ctx.enter_context(tc.psum_pool(name="psum", bufs=1))
 
-        gather_list = sb.tile([P, S // 16], U16, name="gather_list")
-        scatter_list = sb.tile([P, S // 16], U16, name="scatter_list")
-        wgt_sb = sb.tile([P, S], F32, name="wgt_sb")
-        wgo_sb = sb.tile([P, S], F32, name="wgo_sb")
-        planes = [sb.tile([P, T], F32, name=f"plane{i}") for i in range(PACK)]
-        windows = [sb.tile([P, T], F32, name=f"window{t}") for t in range(M // P)]
-        w4_sb = sb.tile([P, 2 * M], U8, name="w4_sb", align_bytes=64)
-        w4_scale = sb.tile([P, M], U8, name="w4_scale", align_bytes=64)
-        bias = sb.tile([P, M // P], F32, name="bias")
-        bias_rows = sb.tile([P, P], F32, name="bias_rows")
-        identity = sb.tile([P, P], F32, name="identity")
-        warm = sb.tile([P, 8], F32, name="warm")
-        warm_out = sb.tile([P, 8], F32, name="warm_out")
-
-        def raw_tile(name, width):
-            return sb.tile([P, PACK, width], F32, name=name, tag=name, align_bytes=64)
-
-        def operand(name, width):
-            return {
-                "codes": sb.tile([P, width], U32, name=name + "_codes", align_bytes=64),
-                "scale": sb.tile([P, width], U8, name=name + "_scale", align_bytes=64),
-            }
-
-        def columns(op, cols):
-            return {"codes": op["codes"][:, cols], "scale": op["scale"][:, cols]}
-
-        xg_raw = raw_tile("xg_raw", S)
-        c_raw = [raw_tile(f"c{h}_raw", HALF) for h in range(2)]
-        u_raw = [raw_tile(f"u{h}_raw", HALF) for h in range(2)]
-        xg, cq, uq = operand("xg", S), operand("cq", S), operand("uq", M)
-        xg_codes = {q: xg["codes"][:, q * N_PASS : (q + 1) * N_PASS] for q in (0, 3)}
-        held_bias = [sb.tile([P, 1], F32, name=f"held_bias{n}", tag=f"held_bias{n}", align_bytes=64) for n in range(3)]
-
-        x_rows = xT.rearrange("(p i) t -> p i t", i=PACK)
-        c_rows = c.rearrange("(p i) j -> p i j", i=PACK)
-        u_rows = u.rearrange("(p i) n -> p i n", i=PACK)
-
         def half(h):
             return slice(h * HALF, (h + 1) * HALF)
+
+        def quarter(q):
+            return slice(q * QUARTER, (q + 1) * QUARTER)
 
         def rows(t):
             return slice(P * t, P * (t + 1))
 
         def listed(cols):
-            return slice(cols.start // 16, cols.stop // 16)
-
-        def quarter(q):
-            return slice(q * N_PASS, (q + 1) * N_PASS)
+            return slice(cols.start // GROUP, cols.stop // GROUP)
 
         whole = slice(0, S)
+        middle = slice(QUARTER, 3 * QUARTER)
+
+        def raw_tile(name, width):
+            return sb.tile([P, PACK, width], F32, name=name, tag=name, align_bytes=MX_ALIGN)
+
+        def grouped_tile(name, width, tag=None):
+            return sb.tile([P, width, PACK], BF16, name=name, tag=tag or name, align_bytes=MX_ALIGN)
+
+        def codes_tile(name, width, tag=None):
+            return sb.tile([P, width], U32, name=name, tag=tag or name, align_bytes=MX_ALIGN)
+
+        def scale_tile(name, width):
+            return sb.tile([P, width], U8, name=name, align_bytes=MX_ALIGN)
+
+        gather_list = sb.tile([P, S // GROUP], U16, name="gather_list")
+        scatter_list = sb.tile([P, S // GROUP], U16, name="scatter_list")
+        wgt_sb = sb.tile([P, S], F32, name="wgt_sb")
+        wgo_sb = sb.tile([P, S], F32, name="wgo_sb")
+        planes = [sb.tile([P, T], F32, name=f"plane{i}") for i in range(PACK)]
+        windows = [sb.tile([P, T], F32, name=f"window{t}") for t in range(ROW_TILES)]
+        w4_sb = sb.tile([P, 2 * M], U8, name="w4_sb", align_bytes=MX_ALIGN)
+        w4_scale = scale_tile("w4_scale", M)
+        bias_rows = sb.tile([P, P], F32, name="bias_rows")
+        identity = sb.tile([P, P], F32, name="identity")
+        warm = sb.tile([P, 8], F32, name="warm")
+        warm_out = sb.tile([P, 8], F32, name="warm_out")
+        xg_raw = raw_tile("xg_raw", S)
+        c_raw = [raw_tile(f"c_half{h}_raw", HALF) for h in range(2)]
+        u_raw = [raw_tile(f"u_half{h}_raw", HALF) for h in range(2)]
+        xg_codes = {q: codes_tile(f"xg{q}_codes", QUARTER)[:] for q in (0, 3)}
+        xg_scale = scale_tile("xg_scale", S)
+        c_codes, c_scale = codes_tile("c_codes", S), scale_tile("c_scale", S)
+        u_codes, u_scale = codes_tile("u_codes", M), scale_tile("u_scale", M)
+        first_bias = [sb.tile([P, 1], F32, name=f"first_bias{n}", tag=f"first_bias{n}", align_bytes=MX_ALIGN) for n in range(3)]
+        later_bias = sb.tile([P, ROW_TILES - 1], F32, name="later_bias")
 
         nc.gpsimd.memset(w4_scale[:].bitcast(I32), 0)
         nc.gpsimd.memset(bias_rows[:], 0.0)
@@ -86,15 +89,21 @@ def tile_list_hboth_d_silu_kernel(tc, xT, w4_words, w4_scales, c, u, wgt, b, wgo
         nc.scalar.activation(warm_out[:], warm[:], SILU)
         make_identity(nc, identity[:])
 
+        x_rows = xT.rearrange("(p i) t -> p i t", i=PACK)
+        c_rows = c.rearrange("(p i) j -> p i j", i=PACK)
+        u_rows = u.rearrange("(p i) n -> p i n", i=PACK)
         nc.sync.dma_start(gather_list[:], offs)
         nc.sync.dma_start(wgt_sb[:, half(0)], wgt[:, half(0)])
         nc.sync.dma_start(planes[0][:], x_rows[:, 0, :])
         nc.sync.dma_start(wgt_sb[:, half(1)], wgt[:, half(1)])
         for i in range(1, PACK - 1):
             nc.sync.dma_start(planes[i][:], x_rows[:, i, :])
-        nc.sync.dma_start(bias_rows[0 : M // P, :], b.rearrange("(t p) -> t p", p=P))
-        for q in range(4):
-            nc.sync.dma_start(w4_scale[32 * q : 32 * q + 4, :].bitcast(I32), w4_scales[0, 4 * q : 4 * q + 4, :].bitcast(I32))
+        nc.sync.dma_start(bias_rows[0:ROW_TILES, :], b.rearrange("(t p) -> t p", p=P))
+        for quadrant in range(4):
+            nc.sync.dma_start(
+                w4_scale[32 * quadrant : 32 * quadrant + 4, :].bitcast(I32),
+                w4_scales[0, 4 * quadrant : 4 * quadrant + 4, :].bitcast(I32),
+            )
         nc.sync.dma_start(planes[PACK - 1][:], x_rows[:, PACK - 1, :])
         nc.sync.dma_start(u_raw[0][:], u_rows[:, :, half(0)])
         nc.sync.dma_start(c_raw[0][:], c_rows[:, :, half(0)])
@@ -102,39 +111,38 @@ def tile_list_hboth_d_silu_kernel(tc, xT, w4_words, w4_scales, c, u, wgt, b, wgo
         nc.sync.dma_start(scatter_list[:], offs2)
         nc.sync.dma_start(wgo_sb[:, quarter(0)], wgo[:, quarter(0)])
         nc.sync.dma_start(c_raw[1][:], c_rows[:, :, half(1)])
-        nc.sync.dma_start(wgo_sb[:, N_PASS:S], wgo[:, N_PASS:S])
+        nc.sync.dma_start(wgo_sb[:, QUARTER:S], wgo[:, QUARTER:S])
         nc.sync.dma_start(u_raw[1][:], u_rows[:, :, half(1)])
 
         bias_ps = psum.tile([P, P], F32, name="bias_ps", tag="bias_ps")
         nc.tensor.transpose(bias_ps[:], bias_rows[:], identity[:])
-        nc.scalar.copy(bias[:], bias_ps[:, 0 : M // P])
-        for column, t in zip(held_bias, (0, 0, 0)):
-            nc.scalar.copy(column[:], bias_ps[:, t : t + 1])
+        nc.scalar.copy(later_bias[:], bias_ps[:, 1:ROW_TILES])
+        for column in first_bias:
+            nc.scalar.copy(column[:], bias_ps[:, 0:1])
 
         for window in windows[:2]:
             nc.vector.memset(window[:], 0.0)
         for window in windows[2:]:
             nc.gpsimd.memset(window[:], 0.0)
 
+        on_scalar, on_vector = nc.scalar.copy, nc.vector.tensor_copy
+
         def gather(i, cols):
             nc.vector.tensor_tensor(xg_raw[:, i, cols], planes[i][:].indirect(gather_list[:, listed(cols)]), wgt_sb[:, cols], MULT)
 
-        def bf16_tile(name, width, tag=None):
-            return sb.tile([P, width, PACK], BF16, name=name, tag=tag or name, align_bytes=64)
-
         def interleave(copy, grouped, raw):
-            copy(grouped.rearrange("p (c r) i -> p c i r", r=4), raw.rearrange("p i (c r) -> p c i r", r=4))
+            copy(grouped.rearrange("p (c r) i -> p c i r", r=RUN), raw.rearrange("p i (c r) -> p c i r", r=RUN))
 
-        def quantize(op, grouped):
-            nc.vector.quantize_mx(out=op["codes"].bitcast(FP8X4), scales=op["scale"], in_=grouped.rearrange("p w i -> p (w i)"))
+        def quantize(codes, scale, grouped):
+            nc.vector.quantize_mx(out=codes.bitcast(FP8X4), scales=scale, in_=grouped.rearrange("p w i -> p (w i)"))
 
-        def w4_pass(acc, t, cols, start, stop):
+        def w4_pass(acc, t, q, start, stop):
             nc.tensor.matmul_mx(
                 out=acc,
                 lhsT=w4_sb[:, 2 * P * t : 2 * P * (t + 1)].bitcast(FP4X4),
                 lhsT_scale=w4_scale[:, rows(t)],
-                rhs=xg_codes[cols.start // N_PASS].bitcast(FP8X4),
-                rhs_scale=xg["scale"][:, cols],
+                rhs=xg_codes[q].bitcast(FP8X4),
+                rhs_scale=xg_scale[:, quarter(q)],
                 start=start,
                 stop=stop,
             )
@@ -142,28 +150,31 @@ def tile_list_hboth_d_silu_kernel(tc, xT, w4_words, w4_scales, c, u, wgt, b, wgo
         def u_pass(acc, t, cols, start, stop):
             nc.tensor.matmul_mx(
                 out=acc,
-                lhsT=uq["codes"][:, rows(t)].bitcast(FP8X4),
-                lhsT_scale=uq["scale"][:, rows(t)],
-                rhs=cq["codes"][:, cols].bitcast(FP8X4),
-                rhs_scale=cq["scale"][:, cols],
+                lhsT=u_codes[:, rows(t)].bitcast(FP8X4),
+                lhsT_scale=u_scale[:, rows(t)],
+                rhs=c_codes[:, cols].bitcast(FP8X4),
+                rhs_scale=c_scale[:, cols],
                 start=start,
                 stop=stop,
             )
 
         def project(t, cols, bank, bias_column, w4_first, tag=None):
             width = cols.stop - cols.start
-            step = N_PASS
+            count = width // QUARTER
             acc = psum.tile([P, width], F32, name=f"acc{t}_{cols.start}", tag=bank)
             if not w4_first:
                 u_pass(acc[:], t, cols, True, False)
-            for at in range(0, width, step):
-                w4_pass(acc[:, at : at + step], t, slice(cols.start + at, cols.start + at + step), w4_first and at == 0, not w4_first and at + step == width)
+            for n in range(count):
+                w4_pass(acc[:, quarter(n)], t, cols.start // QUARTER + n, w4_first and n == 0, not w4_first and n == count - 1)
             if w4_first:
                 u_pass(acc[:], t, cols, False, True)
             name = f"act{t}_{cols.start}"
-            act = sb.tile([P, width], F32, name=name, tag=tag or name, align_bytes=64)
+            act = sb.tile([P, width], F32, name=name, tag=tag or name, align_bytes=MX_ALIGN)
             nc.scalar.activation(act[:], acc[:], SILU, bias=bias_column)
             return act
+
+        def bias_of(t):
+            return later_bias[:, t - 1 : t]
 
         def scatter(t, cols, act):
             nc.vector.tensor_tensor(windows[t][:].indirect(scatter_list[:, listed(cols)]), act[:], wgo_sb[:, cols], MULT)
@@ -171,62 +182,66 @@ def tile_list_hboth_d_silu_kernel(tc, xT, w4_words, w4_scales, c, u, wgt, b, wgo
         def store(t):
             nc.sync.dma_start(out[rows(t), :], windows[t][:])
 
-        on_scalar, on_vector = nc.scalar.copy, nc.vector.tensor_copy
         for h in range(2):
             gather(0, half(h))
         gather(1, whole)
-        middle = slice(N_PASS, 3 * N_PASS)
-        xg_bf = [bf16_tile("xg0_bf", N_PASS), bf16_tile("xg12_bf", HALF)]
-        interleave(on_scalar, xg_bf[0][:, :, 0:2], xg_raw[:, 0:2, quarter(0)])
-        interleave(on_scalar, xg_bf[1][:, :, 0:2], xg_raw[:, 0:2, middle])
+        xg0_bf, xg_middle_bf = grouped_tile("xg0_bf", QUARTER), grouped_tile("xg_middle_bf", HALF)
+        interleave(on_scalar, xg0_bf[:, :, 0:2], xg_raw[:, 0:2, quarter(0)])
+        interleave(on_scalar, xg_middle_bf[:, :, 0:2], xg_raw[:, 0:2, middle])
         gather(2, whole)
         for cols in (quarter(0), middle, quarter(3)):
             gather(PACK - 1, cols)
-        u_bf = [bf16_tile(f"u{t}_bf", P) for t in range(2)]
-        c_bf = [bf16_tile(f"c{q}_bf", N_PASS) for q in range(2)]
-        interleave(on_scalar, xg_bf[0][:, :, 2:4], xg_raw[:, 2:4, quarter(0)])
-        interleave(on_vector, xg_bf[1][:, :, 2:4], xg_raw[:, 2:4, middle])
+
+        u_bf = [grouped_tile(f"u{t}_bf", P) for t in range(2)]
+        c_bf = [grouped_tile(f"c{q}_bf", QUARTER) for q in range(2)]
+        interleave(on_scalar, xg0_bf[:, :, 2:4], xg_raw[:, 2:4, quarter(0)])
+        interleave(on_vector, xg_middle_bf[:, :, 2:4], xg_raw[:, 2:4, middle])
         for t in range(2):
             interleave(on_scalar, u_bf[t][:], u_raw[0][:, :, rows(t)])
-        quantize(columns(xg, quarter(0)), xg_bf[0][:])
-        quantize(columns(uq, rows(0)), u_bf[0][:])
+        quantize(xg_codes[0], xg_scale[:, quarter(0)], xg0_bf[:])
+        quantize(u_codes[:, rows(0)], u_scale[:, rows(0)], u_bf[0][:])
         interleave(on_vector, c_bf[0][:], c_raw[0][:, :, quarter(0)])
         interleave(on_scalar, c_bf[1][:], c_raw[0][:, :, quarter(1)])
-        quantize(columns(uq, rows(1)), u_bf[1][:])
-        quantize(columns(cq, quarter(0)), c_bf[0][:])
-        act0 = project(0, quarter(0), "bank0", held_bias[0][:], True)
-        act1 = project(1, quarter(0), "bank1", bias[:, 1:2], True)
-        xg_late_bf = bf16_tile("xg_late_bf", N_PASS, tag="u1_bf")
-        interleave(on_vector, xg_late_bf[:, 0:64, :], xg_raw[:, :, 3 * N_PASS : 3 * N_PASS + 64])
-        interleave(on_scalar, xg_late_bf[:, 64:P, :], xg_raw[:, :, 3 * N_PASS + 64 : S])
-        middle_codes = sb.tile([P, HALF], U32, name="middle_codes", tag="c0_bf", align_bytes=64)
+        quantize(u_codes[:, rows(1)], u_scale[:, rows(1)], u_bf[1][:])
+        quantize(c_codes[:, quarter(0)], c_scale[:, quarter(0)], c_bf[0][:])
+        act0 = project(0, quarter(0), "bank0", first_bias[0][:], True)
+        act1 = project(1, quarter(0), "bank1", bias_of(1), True)
+
+        xg3_bf = grouped_tile("xg3_bf", QUARTER, tag="u1_bf")
+        split = 3 * QUARTER + LAST_ON_VECTOR
+        interleave(on_vector, xg3_bf[:, 0:LAST_ON_VECTOR, :], xg_raw[:, :, 3 * QUARTER : split])
+        interleave(on_scalar, xg3_bf[:, LAST_ON_VECTOR:QUARTER, :], xg_raw[:, :, split:S])
+        middle_codes = codes_tile("xg_middle_codes", HALF, tag="c0_bf")
         xg_codes[1], xg_codes[2] = middle_codes[:, quarter(0)], middle_codes[:, quarter(1)]
-        quantize(columns(cq, quarter(1)), c_bf[1][:])
-        quantize({"codes": middle_codes[:], "scale": xg["scale"][:, middle]}, xg_bf[1][:])
-        quantize(columns(xg, quarter(3)), xg_late_bf[:])
+        quantize(c_codes[:, quarter(1)], c_scale[:, quarter(1)], c_bf[1][:])
+        quantize(middle_codes[:], xg_scale[:, middle], xg_middle_bf[:])
+        quantize(xg_codes[3], xg_scale[:, quarter(3)], xg3_bf[:])
         scatter(0, quarter(0), act0)
         scatter(1, quarter(0), act1)
-        c1_bf = bf16_tile("c_late_bf", HALF, tag="held_bias0")
-        interleave(on_scalar, c1_bf[:], c_raw[1][:])
-        act0 = project(0, quarter(1), "bank2", held_bias[1][:], False, tag="c1_raw")
-        act1 = project(1, quarter(1), "bank3", bias[:, 1:2], False, tag="held_bias1")
-        quantize(columns(cq, half(1)), c1_bf[:])
+
+        c_late_bf = grouped_tile("c_late_bf", HALF, tag="first_bias0")
+        interleave(on_scalar, c_late_bf[:], c_raw[1][:])
+        act0 = project(0, quarter(1), "bank2", first_bias[1][:], False, tag="c_half1_raw")
+        act1 = project(1, quarter(1), "bank3", bias_of(1), False, tag="first_bias1")
+        quantize(c_codes[:, half(1)], c_scale[:, half(1)], c_late_bf[:])
         scatter(0, quarter(1), act0)
         scatter(1, quarter(1), act1)
-        act0 = project(0, half(1), "bank0", held_bias[2][:], True)
-        u23_bf = bf16_tile("u23_bf", HALF, tag="held_bias2")
-        interleave(on_scalar, u23_bf[:], u_raw[1][:])
-        act1 = project(1, half(1), "bank1", bias[:, 1:2], True, tag="u1_raw")
+
+        act0 = project(0, half(1), "bank0", first_bias[2][:], True)
+        u_late_bf = grouped_tile("u_late_bf", HALF, tag="first_bias2")
+        interleave(on_scalar, u_late_bf[:], u_raw[1][:])
+        act1 = project(1, half(1), "bank1", bias_of(1), True, tag="u_half1_raw")
         scatter(0, half(1), act0)
         store(0)
-        quantize(columns(uq, half(1)), u23_bf[:])
+        quantize(u_codes[:, half(1)], u_scale[:, half(1)], u_late_bf[:])
         scatter(1, half(1), act1)
         store(1)
-        act2 = project(2, half(0), "bank2", bias[:, 2:3], True)
-        act3 = project(3, whole, "bank3", bias[:, 3:4], True)
-        last = project(2, half(1), "bank4", bias[:, 2:3], False)
+
+        act2 = project(2, half(0), "bank2", bias_of(2), True)
+        act3 = project(3, whole, "bank3", bias_of(3), True)
+        act2_late = project(2, half(1), "bank4", bias_of(2), False)
         scatter(2, half(0), act2)
         scatter(3, whole, act3)
         store(3)
-        scatter(2, half(1), last)
+        scatter(2, half(1), act2_late)
         store(2)

@@ -92,9 +92,9 @@ def tile_list_hboth_d_silu_kernel(tc, xT, w4_words, w4_scales, c, u, wgt, b, wgo
         x_rows = xT.rearrange("(p i) t -> p i t", i=PACK)
         c_rows = c.rearrange("(p i) j -> p i j", i=PACK)
         u_rows = u.rearrange("(p i) n -> p i n", i=PACK)
+        nc.sync.dma_start(planes[0][:], x_rows[:, 0, :])
         nc.sync.dma_start(gather_list[:], offs)
         nc.sync.dma_start(wgt_sb[:, half(0)], wgt[:, half(0)])
-        nc.sync.dma_start(planes[0][:], x_rows[:, 0, :])
         nc.sync.dma_start(wgt_sb[:, half(1)], wgt[:, half(1)])
         for i in range(1, PACK - 1):
             nc.sync.dma_start(planes[i][:], x_rows[:, i, :])

@@ -99,12 +99,12 @@ def tile_list_hboth_d_silu_kernel(tc, xT, w4_words, w4_scales, c, u, wgt, b, wgo
         for i in range(1, PACK - 1):
             nc.sync.dma_start(planes[i][:], x_rows[:, i, :])
         nc.sync.dma_start(bias_rows[0:ROW_TILES, :], b.rearrange("(t p) -> t p", p=P))
+        nc.sync.dma_start(planes[PACK - 1][:], x_rows[:, PACK - 1, :])
         for quadrant in range(4):
             nc.sync.dma_start(
                 w4_scale[32 * quadrant : 32 * quadrant + 4, :].bitcast(I32),
                 w4_scales[0, 4 * quadrant : 4 * quadrant + 4, :].bitcast(I32),
             )
-        nc.sync.dma_start(planes[PACK - 1][:], x_rows[:, PACK - 1, :])
         nc.sync.dma_start(u_raw[0][:], u_rows[:, :, half(0)])
         nc.sync.dma_start(c_raw[0][:], c_rows[:, :, half(0)])
         nc.sync.dma_start(w4_sb[:].bitcast(I32), w4_words[0].bitcast(I32))

@@ -24,7 +24,7 @@ HALF = S // 2
 QUARTER = S // 4
 GROUP = 16
 RUN = 4
-MX_ALIGN = 64
+MX_ALIGN = 256
 LAST_ON_VECTOR = QUARTER // 2
 
 
@@ -63,10 +63,10 @@ def tile_list_hboth_d_silu_kernel(tc, xT, w4_words, w4_scales, c, u, wgt, b, wgo
 
         gather_list = sb.tile([P, S // GROUP], U16, name="gather_list")
         scatter_list = sb.tile([P, S // GROUP], U16, name="scatter_list")
-        wgt_sb = sb.tile([P, S], F32, name="wgt_sb")
-        wgo_sb = sb.tile([P, S], F32, name="wgo_sb")
-        planes = [sb.tile([P, T], F32, name=f"plane{i}") for i in range(PACK)]
-        windows = [sb.tile([P, T], F32, name=f"window{t}") for t in range(ROW_TILES)]
+        wgt_sb = sb.tile([P, S], F32, name="wgt_sb", align_bytes=MX_ALIGN)
+        wgo_sb = sb.tile([P, S], F32, name="wgo_sb", align_bytes=MX_ALIGN)
+        planes = [sb.tile([P, T], F32, name=f"plane{i}", align_bytes=MX_ALIGN) for i in range(PACK)]
+        windows = [sb.tile([P, T], F32, name=f"window{t}", align_bytes=MX_ALIGN) for t in range(ROW_TILES)]
         w4_sb = sb.tile([P, 2 * M], U8, name="w4_sb", align_bytes=MX_ALIGN)
         w4_scale = scale_tile("w4_scale", M)
         bias_rows = sb.tile([P, P], F32, name="bias_rows")

@@ -74,7 +74,8 @@ def tile_list_hboth_d_silu_kernel(tc, xT, w4_words, w4_scales, c, u, wgt, b, wgo
         warm = sb.tile([P, 8], F32, name="warm")
         warm_out = sb.tile([P, 8], F32, name="warm_out")
         xg_raw = raw_tile("xg_raw", S)
-        c_raw = [raw_tile(f"c_half{h}_raw", HALF) for h in range(2)]
+        c_early_raw = [raw_tile(f"c{q}_raw", QUARTER) for q in range(2)]
+        c_late_raw = raw_tile("c_half1_raw", HALF)
         u_raw = [raw_tile(f"u_half{h}_raw", HALF) for h in range(2)]
         xg_codes = {q: codes_tile(f"xg{q}_codes", QUARTER)[:] for q in (0, 3)}
         xg_scale = scale_tile("xg_scale", S)
@@ -94,8 +95,7 @@ def tile_list_hboth_d_silu_kernel(tc, xT, w4_words, w4_scales, c, u, wgt, b, wgo
         u_rows = u.rearrange("(p i) n -> p i n", i=PACK)
         nc.sync.dma_start(planes[0][:], x_rows[:, 0, :])
         nc.sync.dma_start(gather_list[:], offs)
-        nc.sync.dma_start(wgt_sb[:, half(0)], wgt[:, half(0)])
-        nc.sync.dma_start(wgt_sb[:, half(1)], wgt[:, half(1)])
+        nc.sync.dma_start(wgt_sb[:], wgt)
         for i in range(1, PACK - 1):
             nc.sync.dma_start(planes[i][:], x_rows[:, i, :])
         nc.sync.dma_start(bias_rows[0:ROW_TILES, :], b.rearrange("(t p) -> t p", p=P))
@@ -106,11 +106,12 @@ def tile_list_hboth_d_silu_kernel(tc, xT, w4_words, w4_scales, c, u, wgt, b, wgo
                 w4_scales[0, 4 * quadrant : 4 * quadrant + 4, :].bitcast(I32),
             )
         nc.sync.dma_start(u_raw[0][:], u_rows[:, :, half(0)])
-        nc.sync.dma_start(c_raw[0][:], c_rows[:, :, half(0)])
+        for q in range(2):
+            nc.sync.dma_start(c_early_raw[q][:], c_rows[:, :, quarter(q)])
         nc.sync.dma_start(w4_sb[:].bitcast(I32), w4_words[0].bitcast(I32))
         nc.sync.dma_start(scatter_list[:], offs2)
         nc.sync.dma_start(wgo_sb[:, quarter(0)], wgo[:, quarter(0)])
-        nc.sync.dma_start(c_raw[1][:], c_rows[:, :, half(1)])
+        nc.sync.dma_start(c_late_raw[:], c_rows[:, :, half(1)])
         nc.sync.dma_start(wgo_sb[:, QUARTER:S], wgo[:, QUARTER:S])
         nc.sync.dma_start(u_raw[1][:], u_rows[:, :, half(1)])
 
@@ -182,9 +183,8 @@ def tile_list_hboth_d_silu_kernel(tc, xT, w4_words, w4_scales, c, u, wgt, b, wgo
         def store(t):
             nc.sync.dma_start(out[rows(t), :], windows[t][:])
 
-        for h in range(2):
-            gather(0, half(h))
-        gather(1, whole)
+        for i in range(2):
+            gather(i, whole)
         xg0_bf, xg_middle_bf = grouped_tile("xg0_bf", QUARTER), grouped_tile("xg_middle_bf", HALF)
         interleave(on_scalar, xg0_bf[:, :, 0:2], xg_raw[:, 0:2, quarter(0)])
         interleave(on_scalar, xg_middle_bf[:, :, 0:2], xg_raw[:, 0:2, middle])
@@ -200,8 +200,8 @@ def tile_list_hboth_d_silu_kernel(tc, xT, w4_words, w4_scales, c, u, wgt, b, wgo
             interleave(on_scalar, u_bf[t][:], u_raw[0][:, :, rows(t)])
         quantize(xg_codes[0], xg_scale[:, quarter(0)], xg0_bf[:])
         quantize(u_codes[:, rows(0)], u_scale[:, rows(0)], u_bf[0][:])
-        interleave(on_vector, c_bf[0][:], c_raw[0][:, :, quarter(0)])
-        interleave(on_scalar, c_bf[1][:], c_raw[0][:, :, quarter(1)])
+        interleave(on_vector, c_bf[0][:], c_early_raw[0][:])
+        interleave(on_scalar, c_bf[1][:], c_early_raw[1][:])
         quantize(u_codes[:, rows(1)], u_scale[:, rows(1)], u_bf[1][:])
         quantize(c_codes[:, quarter(0)], c_scale[:, quarter(0)], c_bf[0][:])
         act0 = project(0, quarter(0), "bank0", first_bias[0][:], True)
@@ -220,7 +220,7 @@ def tile_list_hboth_d_silu_kernel(tc, xT, w4_words, w4_scales, c, u, wgt, b, wgo
         scatter(1, quarter(0), act1)
 
         c_late_bf = grouped_tile("c_late_bf", HALF, tag="first_bias0")
-        interleave(on_scalar, c_late_bf[:], c_raw[1][:])
+        interleave(on_scalar, c_late_bf[:], c_late_raw[:])
         act0 = project(0, quarter(1), "bank2", first_bias[1][:], False, tag="c_half1_raw")
         act1 = project(1, quarter(1), "bank3", bias_of(1), False, tag="first_bias1")
         quantize(c_codes[:, half(1)], c_scale[:, half(1)], c_late_bf[:])

@@ -1,7 +1,6 @@
 from contextlib import ExitStack
 
 import concourse.mybir as mybir
-from concourse.masks import make_identity
 
 K, M, T, S = 512, 512, 1024, 512
 FLOPS = 2 * 2 * K * M * S
@@ -26,12 +25,17 @@ GROUP = 16
 RUN = 4
 MX_ALIGN = 256
 LAST_ON_VECTOR = QUARTER // 2
+BLOCK = 32
+PAIR = 2
+HALF_ROW_STEP = GROUP + 1
+BIAS_STEP = BLOCK // ROW_TILES
 
 
 def tile_list_hboth_d_silu_kernel(tc, xT, w4_words, w4_scales, c, u, wgt, b, wgo, offs, offs2, out):
     nc = tc.nc
     with ExitStack() as ctx:
         sb = ctx.enter_context(tc.tile_pool(name="sb", bufs=1))
+        shared = ctx.enter_context(tc.tile_pool(name="shared", bufs=1))
         psum = ctx.enter_context(tc.psum_pool(name="psum", bufs=1))
 
         def half(h):
@@ -66,11 +70,13 @@ def tile_list_hboth_d_silu_kernel(tc, xT, w4_words, w4_scales, c, u, wgt, b, wgo
         wgt_sb = sb.tile([P, S], F32, name="wgt_sb", align_bytes=MX_ALIGN)
         wgo_sb = sb.tile([P, S], F32, name="wgo_sb", align_bytes=MX_ALIGN)
         planes = [sb.tile([P, T], F32, name=f"plane{i}", align_bytes=MX_ALIGN) for i in range(PACK)]
-        windows = [sb.tile([P, T], F32, name=f"window{t}", align_bytes=MX_ALIGN) for t in range(ROW_TILES)]
+        windows = [sb.tile([P, T], F32, name=f"window{t}", align_bytes=MX_ALIGN) for t in range(2)]
         w4_sb = sb.tile([P, 2 * M], U8, name="w4_sb", align_bytes=MX_ALIGN)
         w4_scale = scale_tile("w4_scale", M)
-        bias_rows = sb.tile([P, P], F32, name="bias_rows")
-        identity = sb.tile([P, P], F32, name="identity")
+        wgt_pieces = sb.tile([P, BLOCK], F32, name="wgt_pieces", align_bytes=MX_ALIGN)
+        wgt_turned = sb.tile([P, BLOCK], F32, name="wgt_turned", align_bytes=MX_ALIGN)
+        wgt_repeated = shared.tile([P, S], F32, name="wgt_repeated", align_bytes=MX_ALIGN, offset=3072)
+        bias_pieces = sb.tile([P, BLOCK], F32, name="bias_pieces", align_bytes=MX_ALIGN)
         warm = sb.tile([P, 8], F32, name="warm")
         warm_out = sb.tile([P, 8], F32, name="warm_out")
         xg_raw = raw_tile("xg_raw", S)
@@ -82,29 +88,33 @@ def tile_list_hboth_d_silu_kernel(tc, xT, w4_words, w4_scales, c, u, wgt, b, wgo
         c_codes, c_scale = codes_tile("c_codes", S), scale_tile("c_scale", S)
         u_codes, u_scale = codes_tile("u_codes", M), scale_tile("u_scale", M)
         first_bias = [sb.tile([P, 1], F32, name=f"first_bias{n}", tag=f"first_bias{n}", align_bytes=MX_ALIGN) for n in range(3)]
-        later_bias = sb.tile([P, ROW_TILES - 1], F32, name="later_bias")
 
+        nc.gpsimd.memset(bias_pieces[:], 0.0)
         nc.gpsimd.memset(w4_scale[:].bitcast(I32), 0)
-        nc.gpsimd.memset(bias_rows[:], 0.0)
         nc.gpsimd.memset(warm[:], 0.0)
         nc.scalar.activation(warm_out[:], warm[:], SILU)
-        make_identity(nc, identity[:])
 
         x_rows = xT.rearrange("(p i) t -> p i t", i=PACK)
         c_rows = c.rearrange("(p i) j -> p i j", i=PACK)
         u_rows = u.rearrange("(p i) n -> p i n", i=PACK)
-        nc.sync.dma_start(planes[0][:], x_rows[:, 0, :])
-        nc.sync.dma_start(gather_list[:], offs)
-        nc.sync.dma_start(wgt_sb[:], wgt)
-        for i in range(1, PACK - 1):
-            nc.sync.dma_start(planes[i][:], x_rows[:, i, :])
-        nc.sync.dma_start(bias_rows[0:ROW_TILES, :], b.rearrange("(t p) -> t p", p=P))
-        nc.sync.dma_start(planes[PACK - 1][:], x_rows[:, PACK - 1, :])
-        for quadrant in range(4):
+
+        def load_scale(quadrant):
             nc.sync.dma_start(
                 w4_scale[32 * quadrant : 32 * quadrant + 4, :].bitcast(I32),
                 w4_scales[0, 4 * quadrant : 4 * quadrant + 4, :].bitcast(I32),
             )
+
+        wgt_halves = wgt.rearrange("p (h j) -> (p h) j", h=2)[0 : 2 * P : HALF_ROW_STEP, :]
+        nc.sync.dma_start(wgt_pieces[:], wgt_halves.rearrange("a (e j) -> a e j", j=BLOCK))
+        nc.sync.dma_start(planes[0][:], x_rows[:, 0, :])
+        nc.sync.dma_start(gather_list[:], offs)
+        nc.sync.dma_start(bias_pieces[0:P:BIAS_STEP, :], b.rearrange("(t q j) -> q t j", t=ROW_TILES, j=BLOCK))
+        nc.sync.dma_start(planes[1][:], x_rows[:, 1, :])
+        nc.sync.dma_start(planes[2][:], x_rows[:, 2, :])
+        load_scale(0)
+        nc.sync.dma_start(planes[3][:], x_rows[:, 3, :])
+        for quadrant in range(1, 4):
+            load_scale(quadrant)
         nc.sync.dma_start(u_raw[0][:], u_rows[:, :, half(0)])
         for q in range(2):
             nc.sync.dma_start(c_early_raw[q][:], c_rows[:, :, quarter(q)])
@@ -115,16 +125,26 @@ def tile_list_hboth_d_silu_kernel(tc, xT, w4_words, w4_scales, c, u, wgt, b, wgo
         nc.sync.dma_start(wgo_sb[:, QUARTER:S], wgo[:, QUARTER:S])
         nc.sync.dma_start(u_raw[1][:], u_rows[:, :, half(1)])
 
-        bias_ps = psum.tile([P, P], F32, name="bias_ps", tag="bias_ps")
-        nc.tensor.transpose(bias_ps[:], bias_rows[:], identity[:])
-        nc.scalar.copy(later_bias[:], bias_ps[:, 1:ROW_TILES])
-        for column in first_bias:
-            nc.scalar.copy(column[:], bias_ps[:, 0:1])
+        nc.vector.memset(windows[0][:], 0.0)
+        nc.gpsimd.memset(windows[1][:], 0.0)
 
-        for window in windows[:2]:
-            nc.vector.memset(window[:], 0.0)
-        for window in windows[2:]:
-            nc.gpsimd.memset(window[:], 0.0)
+        nc.vector.transpose(wgt_turned[:], wgt_pieces[:])
+        pieces = wgt_turned[:].rearrange("p (g e) -> p e g", g=PAIR)
+        for h in range(2):
+            nc.vector.tensor_copy(
+                wgt_repeated[:, half(h)].rearrange("p (e g s) -> p e g s", g=PAIR, s=GROUP),
+                pieces[:, 8 * h : 8 * h + 8, :].unsqueeze(3).to_broadcast([P, 8, PAIR, GROUP]),
+            )
+        for h in range(2):
+            nc.vector.transpose(wgt_sb[:, half(h)], wgt_repeated[:, half(h)])
+        for n in range(2):
+            windows.append(shared.tile([P, T], F32, name=f"window{2 + n}", align_bytes=MX_ALIGN, offset=4096 * n))
+            nc.gpsimd.memset(windows[-1][:], 0.0)
+
+        bias = sb.tile([P, BLOCK], F32, name="bias", align_bytes=MX_ALIGN)
+        nc.vector.transpose(bias[:], bias_pieces[:])
+        for column in first_bias:
+            nc.scalar.copy(column[:], bias[:, 0:1])
 
         on_scalar, on_vector = nc.scalar.copy, nc.vector.tensor_copy
 
@@ -175,7 +195,7 @@ def tile_list_hboth_d_silu_kernel(tc, xT, w4_words, w4_scales, c, u, wgt, b, wgo
             return act
 
         def bias_of(t):
-            return later_bias[:, t - 1 : t]
+            return bias[:, BIAS_STEP * t : BIAS_STEP * t + 1]
 
         def scatter(t, cols, act):
             nc.vector.tensor_tensor(windows[t][:].indirect(scatter_list[:, listed(cols)]), act[:], wgo_sb[:, cols], MULT)
@@ -183,8 +203,9 @@ def tile_list_hboth_d_silu_kernel(tc, xT, w4_words, w4_scales, c, u, wgt, b, wgo
         def store(t):
             nc.sync.dma_start(out[rows(t), :], windows[t][:])
 
-        for i in range(2):
-            gather(i, whole)
+        for h in range(2):
+            gather(0, half(h))
+        gather(1, whole)
         xg0_bf, xg_middle_bf = grouped_tile("xg0_bf", QUARTER), grouped_tile("xg_middle_bf", HALF)
         interleave(on_scalar, xg0_bf[:, :, 0:2], xg_raw[:, 0:2, quarter(0)])
         interleave(on_scalar, xg_middle_bf[:, :, 0:2], xg_raw[:, 0:2, middle])

@@ -130,8 +130,8 @@ def tile_list_hboth_d_silu_kernel(tc, xT, w4_words, w4_scales, c, u, wgt, b, wgo
 
         nc.vector.transpose(wgt_turned[:], wgt_pieces[:])
         pieces = wgt_turned[:].rearrange("p (g e) -> p e g", g=PAIR)
-        for h in range(2):
-            nc.vector.tensor_copy(
+        for h, copy in enumerate((nc.vector.tensor_copy, nc.scalar.copy)):
+            copy(
                 wgt_repeated[:, half(h)].rearrange("p (e g s) -> p e g s", g=PAIR, s=GROUP),
                 pieces[:, 8 * h : 8 * h + 8, :].unsqueeze(3).to_broadcast([P, 8, PAIR, GROUP]),
             )

@@ -24,7 +24,7 @@ QUARTER = S // 4
 GROUP = 16
 RUN = 4
 MX_ALIGN = 256
-LAST_ON_VECTOR = QUARTER // 2
+LAST_ON_VECTOR = QUARTER // 4
 BLOCK = 32
 PAIR = 2
 HALF_ROW_STEP = GROUP + 1

@@ -125,8 +125,8 @@ def tile_list_hboth_d_silu_kernel(tc, xT, w4_words, w4_scales, c, u, wgt, b, wgo
         nc.sync.dma_start(wgo_sb[:, QUARTER:S], wgo[:, QUARTER:S])
         nc.sync.dma_start(u_raw[1][:], u_rows[:, :, half(1)])
 
-        nc.vector.memset(windows[0][:], 0.0)
-        nc.gpsimd.memset(windows[1][:], 0.0)
+        for window in windows:
+            nc.vector.memset(window[:], 0.0)
 
         nc.vector.transpose(wgt_turned[:], wgt_pieces[:])
         pieces = wgt_turned[:].rearrange("p (g e) -> p e g", g=PAIR)

from contextlib import ExitStack

import concourse.mybir as mybir

K, M, T, S = 512, 512, 1024, 512
FLOPS = 2 * 2 * K * M * S

F32 = mybir.dt.float32
BF16 = mybir.dt.bfloat16
I32 = mybir.dt.int32
U32 = mybir.dt.uint32
U16 = mybir.dt.uint16
U8 = mybir.dt.uint8
FP8X4 = mybir.dt.float8_e4m3fn_x4
FP4X4 = mybir.dt.float4_e2m1fn_x4
MULT = mybir.AluOpType.mult
SILU = mybir.ActivationFunctionType.Silu

P = 128
PACK = 4
ROW_TILES = M // P
HALF = S // 2
QUARTER = S // 4
GROUP = 16
RUN = 4
MX_ALIGN = 256
LAST_ON_VECTOR = QUARTER // 4
BLOCK = 32
PAIR = 2
HALF_ROW_STEP = GROUP + 1
BIAS_STEP = BLOCK // ROW_TILES


def tile_list_hboth_d_silu_kernel(tc, xT, w4_words, w4_scales, c, u, wgt, b, wgo, offs, offs2, out):
    nc = tc.nc
    with ExitStack() as ctx:
        sb = ctx.enter_context(tc.tile_pool(name="sb", bufs=1))
        shared = ctx.enter_context(tc.tile_pool(name="shared", bufs=1))
        psum = ctx.enter_context(tc.psum_pool(name="psum", bufs=1))

        def half(h):
            return slice(h * HALF, (h + 1) * HALF)

        def quarter(q):
            return slice(q * QUARTER, (q + 1) * QUARTER)

        def rows(t):
            return slice(P * t, P * (t + 1))

        def listed(cols):
            return slice(cols.start // GROUP, cols.stop // GROUP)

        whole = slice(0, S)
        middle = slice(QUARTER, 3 * QUARTER)

        def raw_tile(name, width):
            return sb.tile([P, PACK, width], F32, name=name, tag=name, align_bytes=MX_ALIGN)

        def grouped_tile(name, width, tag=None):
            return sb.tile([P, width, PACK], BF16, name=name, tag=tag or name, align_bytes=MX_ALIGN)

        def codes_tile(name, width, tag=None):
            return sb.tile([P, width], U32, name=name, tag=tag or name, align_bytes=MX_ALIGN)

        def scale_tile(name, width):
            return sb.tile([P, width], U8, name=name, align_bytes=MX_ALIGN)

        gather_list = sb.tile([P, S // GROUP], U16, name="gather_list")
        scatter_list = sb.tile([P, S // GROUP], U16, name="scatter_list")
        wgt_sb = sb.tile([P, S], F32, name="wgt_sb", align_bytes=MX_ALIGN)
        wgo_sb = sb.tile([P, S], F32, name="wgo_sb", align_bytes=MX_ALIGN)
        planes = [sb.tile([P, T], F32, name=f"plane{i}", align_bytes=MX_ALIGN) for i in range(PACK)]
        windows = [sb.tile([P, T], F32, name=f"window{t}", align_bytes=MX_ALIGN) for t in range(2)]
        w4_sb = sb.tile([P, 2 * M], U8, name="w4_sb", align_bytes=MX_ALIGN)
        w4_scale = scale_tile("w4_scale", M)
        wgt_pieces = sb.tile([P, BLOCK], F32, name="wgt_pieces", align_bytes=MX_ALIGN)
        wgt_turned = sb.tile([P, BLOCK], F32, name="wgt_turned", align_bytes=MX_ALIGN)
        wgt_repeated = shared.tile([P, S], F32, name="wgt_repeated", align_bytes=MX_ALIGN, offset=3072)
        bias_pieces = sb.tile([P, BLOCK], F32, name="bias_pieces", align_bytes=MX_ALIGN)
        warm = sb.tile([P, 8], F32, name="warm")
        warm_out = sb.tile([P, 8], F32, name="warm_out")
        xg_raw = raw_tile("xg_raw", S)
        c_early_raw = [raw_tile(f"c{q}_raw", QUARTER) for q in range(2)]
        c_late_raw = raw_tile("c_half1_raw", HALF)
        u_raw = [raw_tile(f"u_half{h}_raw", HALF) for h in range(2)]
        xg_codes = {q: codes_tile(f"xg{q}_codes", QUARTER)[:] for q in (0, 3)}
        xg_scale = scale_tile("xg_scale", S)
        c_codes, c_scale = codes_tile("c_codes", S), scale_tile("c_scale", S)
        u_codes, u_scale = codes_tile("u_codes", M), scale_tile("u_scale", M)
        first_bias = [sb.tile([P, 1], F32, name=f"first_bias{n}", tag=f"first_bias{n}", align_bytes=MX_ALIGN) for n in range(3)]

        nc.gpsimd.memset(bias_pieces[:], 0.0)
        nc.gpsimd.memset(w4_scale[:].bitcast(I32), 0)
        nc.gpsimd.memset(warm[:], 0.0)
        nc.scalar.activation(warm_out[:], warm[:], SILU)

        x_rows = xT.rearrange("(p i) t -> p i t", i=PACK)
        c_rows = c.rearrange("(p i) j -> p i j", i=PACK)
        u_rows = u.rearrange("(p i) n -> p i n", i=PACK)

        def load_scale(quadrant):
            nc.sync.dma_start(
                w4_scale[32 * quadrant : 32 * quadrant + 4, :].bitcast(I32),
                w4_scales[0, 4 * quadrant : 4 * quadrant + 4, :].bitcast(I32),
            )

        wgt_halves = wgt.rearrange("p (h j) -> (p h) j", h=2)[0 : 2 * P : HALF_ROW_STEP, :]
        nc.sync.dma_start(wgt_pieces[:], wgt_halves.rearrange("a (e j) -> a e j", j=BLOCK))
        nc.sync.dma_start(planes[0][:], x_rows[:, 0, :])
        nc.sync.dma_start(gather_list[:], offs)
        nc.sync.dma_start(bias_pieces[0:P:BIAS_STEP, :], b.rearrange("(t q j) -> q t j", t=ROW_TILES, j=BLOCK))
        nc.sync.dma_start(planes[1][:], x_rows[:, 1, :])
        nc.sync.dma_start(planes[2][:], x_rows[:, 2, :])
        load_scale(0)
        nc.sync.dma_start(planes[3][:], x_rows[:, 3, :])
        for quadrant in range(1, 4):
            load_scale(quadrant)
        nc.sync.dma_start(u_raw[0][:], u_rows[:, :, half(0)])
        for q in range(2):
            nc.sync.dma_start(c_early_raw[q][:], c_rows[:, :, quarter(q)])
        nc.sync.dma_start(w4_sb[:].bitcast(I32), w4_words[0].bitcast(I32))
        nc.sync.dma_start(scatter_list[:], offs2)
        nc.sync.dma_start(wgo_sb[:, quarter(0)], wgo[:, quarter(0)])
        nc.sync.dma_start(c_late_raw[:], c_rows[:, :, half(1)])
        nc.sync.dma_start(wgo_sb[:, QUARTER:S], wgo[:, QUARTER:S])
        nc.sync.dma_start(u_raw[1][:], u_rows[:, :, half(1)])

        for window in windows:
            nc.vector.memset(window[:], 0.0)

        nc.vector.transpose(wgt_turned[:], wgt_pieces[:])
        pieces = wgt_turned[:].rearrange("p (g e) -> p e g", g=PAIR)
        for h, copy in enumerate((nc.vector.tensor_copy, nc.scalar.copy)):
            copy(
                wgt_repeated[:, half(h)].rearrange("p (e g s) -> p e g s", g=PAIR, s=GROUP),
                pieces[:, 8 * h : 8 * h + 8, :].unsqueeze(3).to_broadcast([P, 8, PAIR, GROUP]),
            )
        for h in range(2):
            nc.vector.transpose(wgt_sb[:, half(h)], wgt_repeated[:, half(h)])
        for n in range(2):
            windows.append(shared.tile([P, T], F32, name=f"window{2 + n}", align_bytes=MX_ALIGN, offset=4096 * n))
            nc.gpsimd.memset(windows[-1][:], 0.0)

        bias = sb.tile([P, BLOCK], F32, name="bias", align_bytes=MX_ALIGN)
        nc.vector.transpose(bias[:], bias_pieces[:])
        for column in first_bias:
            nc.scalar.copy(column[:], bias[:, 0:1])

        on_scalar, on_vector = nc.scalar.copy, nc.vector.tensor_copy

        def gather(i, cols):
            nc.vector.tensor_tensor(xg_raw[:, i, cols], planes[i][:].indirect(gather_list[:, listed(cols)]), wgt_sb[:, cols], MULT)

        def interleave(copy, grouped, raw):
            copy(grouped.rearrange("p (c r) i -> p c i r", r=RUN), raw.rearrange("p i (c r) -> p c i r", r=RUN))

        def quantize(codes, scale, grouped):
            nc.vector.quantize_mx(out=codes.bitcast(FP8X4), scales=scale, in_=grouped.rearrange("p w i -> p (w i)"))

        def w4_pass(acc, t, q, start, stop):
            nc.tensor.matmul_mx(
                out=acc,
                lhsT=w4_sb[:, 2 * P * t : 2 * P * (t + 1)].bitcast(FP4X4),
                lhsT_scale=w4_scale[:, rows(t)],
                rhs=xg_codes[q].bitcast(FP8X4),
                rhs_scale=xg_scale[:, quarter(q)],
                start=start,
                stop=stop,
            )

        def u_pass(acc, t, cols, start, stop):
            nc.tensor.matmul_mx(
                out=acc,
                lhsT=u_codes[:, rows(t)].bitcast(FP8X4),
                lhsT_scale=u_scale[:, rows(t)],
                rhs=c_codes[:, cols].bitcast(FP8X4),
                rhs_scale=c_scale[:, cols],
                start=start,
                stop=stop,
            )

        def project(t, cols, bank, bias_column, w4_first, tag=None):
            width = cols.stop - cols.start
            count = width // QUARTER
            acc = psum.tile([P, width], F32, name=f"acc{t}_{cols.start}", tag=bank)
            if not w4_first:
                u_pass(acc[:], t, cols, True, False)
            for n in range(count):
                w4_pass(acc[:, quarter(n)], t, cols.start // QUARTER + n, w4_first and n == 0, not w4_first and n == count - 1)
            if w4_first:
                u_pass(acc[:], t, cols, False, True)
            name = f"act{t}_{cols.start}"
            act = sb.tile([P, width], F32, name=name, tag=tag or name, align_bytes=MX_ALIGN)
            nc.scalar.activation(act[:], acc[:], SILU, bias=bias_column)
            return act

        def bias_of(t):
            return bias[:, BIAS_STEP * t : BIAS_STEP * t + 1]

        def scatter(t, cols, act):
            nc.vector.tensor_tensor(windows[t][:].indirect(scatter_list[:, listed(cols)]), act[:], wgo_sb[:, cols], MULT)

        def store(t):
            nc.sync.dma_start(out[rows(t), :], windows[t][:])

        for h in range(2):
            gather(0, half(h))
        gather(1, whole)
        xg0_bf, xg_middle_bf = grouped_tile("xg0_bf", QUARTER), grouped_tile("xg_middle_bf", HALF)
        interleave(on_scalar, xg0_bf[:, :, 0:2], xg_raw[:, 0:2, quarter(0)])
        interleave(on_scalar, xg_middle_bf[:, :, 0:2], xg_raw[:, 0:2, middle])
        gather(2, whole)
        for cols in (quarter(0), middle, quarter(3)):
            gather(PACK - 1, cols)

        u_bf = [grouped_tile(f"u{t}_bf", P) for t in range(2)]
        c_bf = [grouped_tile(f"c{q}_bf", QUARTER) for q in range(2)]
        interleave(on_scalar, xg0_bf[:, :, 2:4], xg_raw[:, 2:4, quarter(0)])
        interleave(on_vector, xg_middle_bf[:, :, 2:4], xg_raw[:, 2:4, middle])
        for t in range(2):
            interleave(on_scalar, u_bf[t][:], u_raw[0][:, :, rows(t)])
        quantize(xg_codes[0], xg_scale[:, quarter(0)], xg0_bf[:])
        quantize(u_codes[:, rows(0)], u_scale[:, rows(0)], u_bf[0][:])
        interleave(on_vector, c_bf[0][:], c_early_raw[0][:])
        interleave(on_scalar, c_bf[1][:], c_early_raw[1][:])
        quantize(u_codes[:, rows(1)], u_scale[:, rows(1)], u_bf[1][:])
        quantize(c_codes[:, quarter(0)], c_scale[:, quarter(0)], c_bf[0][:])
        act0 = project(0, quarter(0), "bank0", first_bias[0][:], True)
        act1 = project(1, quarter(0), "bank1", bias_of(1), True)

        xg3_bf = grouped_tile("xg3_bf", QUARTER, tag="u1_bf")
        split = 3 * QUARTER + LAST_ON_VECTOR
        interleave(on_vector, xg3_bf[:, 0:LAST_ON_VECTOR, :], xg_raw[:, :, 3 * QUARTER : split])
        interleave(on_scalar, xg3_bf[:, LAST_ON_VECTOR:QUARTER, :], xg_raw[:, :, split:S])
        middle_codes = codes_tile("xg_middle_codes", HALF, tag="c0_bf")
        xg_codes[1], xg_codes[2] = middle_codes[:, quarter(0)], middle_codes[:, quarter(1)]
        quantize(c_codes[:, quarter(1)], c_scale[:, quarter(1)], c_bf[1][:])
        quantize(middle_codes[:], xg_scale[:, middle], xg_middle_bf[:])
        quantize(xg_codes[3], xg_scale[:, quarter(3)], xg3_bf[:])
        scatter(0, quarter(0), act0)
        scatter(1, quarter(0), act1)

        c_late_bf = grouped_tile("c_late_bf", HALF, tag="first_bias0")
        interleave(on_scalar, c_late_bf[:], c_late_raw[:])
        act0 = project(0, quarter(1), "bank2", first_bias[1][:], False, tag="c_half1_raw")
        act1 = project(1, quarter(1), "bank3", bias_of(1), False, tag="first_bias1")
        quantize(c_codes[:, half(1)], c_scale[:, half(1)], c_late_bf[:])
        scatter(0, quarter(1), act0)
        scatter(1, quarter(1), act1)

        act0 = project(0, half(1), "bank0", first_bias[2][:], True)
        u_late_bf = grouped_tile("u_late_bf", HALF, tag="first_bias2")
        interleave(on_scalar, u_late_bf[:], u_raw[1][:])
        act1 = project(1, half(1), "bank1", bias_of(1), True, tag="u_half1_raw")
        scatter(0, half(1), act0)
        store(0)
        quantize(u_codes[:, half(1)], u_scale[:, half(1)], u_late_bf[:])
        scatter(1, half(1), act1)
        store(1)

        act2 = project(2, half(0), "bank2", bias_of(2), True)
        act3 = project(3, whole, "bank3", bias_of(3), True)
        act2_late = project(2, half(1), "bank4", bias_of(2), False)
        scatter(2, half(0), act2)
        scatter(3, whole, act3)
        store(3)
        scatter(2, half(1), act2_late)
        store(2)
